import numpy as np
import ml_dtypes


def mxq(x, axis, fmt="e4m3"):
    dtype, down = {"e4m3": (ml_dtypes.float8_e4m3fn, 7), "e5m2": (ml_dtypes.float8_e5m2, 14)}[fmt]
    v = np.moveaxis(np.asarray(x, np.float32).astype(ml_dtypes.bfloat16).astype(np.float64), axis, -1)
    blocks = v.reshape(v.shape[:-1] + (-1, 32))
    amax = np.abs(blocks).max(-1, keepdims=True)
    byte = np.maximum(np.where(amax > 0, np.frexp(amax)[1] - 1 + 127, 0) - down, 1)
    scale = np.exp2(byte - 127.0)
    codes = (blocks / scale).astype(np.float32).astype(dtype).astype(np.float64)
    return np.moveaxis((codes * scale).reshape(v.shape), -1, axis)


WIDE = False


def mx_kscale(k):
    if not WIDE:
        return np.ones(k)
    levels = np.array([24, -24, 12, -12, 0])
    if k % 512:
        return np.exp2(np.random.permutation(np.resize(levels, k // 32))).repeat(32)
    a = np.empty((k // 512, 16))
    for p in range(k // 512):
        a[p, :8] = np.random.permutation(np.resize(levels, 8))
        for g in range(8):
            far = levels[np.abs(levels - a[p, g]) >= 10]
            a[p, g + 8] = far[np.random.randint(len(far))]
    return np.exp2(a.ravel()).repeat(32)


def f64(x):
    return np.asarray(x).astype(np.float64)


def striped(idx):
    return np.tile(idx.reshape(-1, 16).T, (8, 1)).astype(np.uint16)


def unstriped(offs):
    return offs[:16].T.reshape(-1).astype(np.int64)


E2M1 = np.array([0.0, 0.5, 1.0, 1.5, 2.0, 3.0, 4.0, 6.0, -0.0, -0.5, -1.0, -1.5, -2.0, -3.0, -4.0, -6.0])


def pack_weight(w, fmt):
    k, n = w.shape
    w = f64(np.asarray(w, np.float32).astype(ml_dtypes.bfloat16)).reshape(k // 32, 32, n)
    amax = np.abs(w).max(1)
    if fmt == "e4m3":
        byte = np.frexp(amax)[1] - 1 + 127 - 7
    else:
        mant, ex = np.frexp(amax / 6.0)
        byte = np.where(mant > 0.5, ex, ex - 1) + 127
    byte = np.clip(np.where(amax > 0, byte, 1), 1, 254)
    scaled = (w * np.exp2(127.0 - byte)[:, None, :]).reshape(k, n).astype(np.float32)
    by_word = np.ascontiguousarray(scaled.reshape(k // 512, 128, 4, n).transpose(0, 1, 3, 2))
    if fmt == "e4m3":
        words = by_word.astype(ml_dtypes.float8_e4m3fn).view(np.uint8)
    else:
        c = by_word.astype(ml_dtypes.float4_e2m1fn).view(np.uint8) & 0xF
        words = (c[..., 0::2] | (c[..., 1::2] << 4)).reshape(k // 512, 128, 2 * n)
    return np.ascontiguousarray(words), np.ascontiguousarray(byte.astype(np.uint8).reshape(k // 512, 16, n))


def unpack_weight(words, scales, fmt):
    g, _, n = scales.shape
    words = np.ascontiguousarray(words).reshape(g, 128, n, -1)
    if fmt == "e4m3":
        vals = words.view(ml_dtypes.float8_e4m3fn).astype(np.float64)
    else:
        nib = np.empty((g, 128, n, 4), np.uint8)
        nib[..., 0::2] = words & 0xF
        nib[..., 1::2] = words >> 4
        vals = E2M1[nib]
    vals = vals * np.repeat(np.exp2(scales.astype(np.float64) - 127.0), 8, axis=1)[..., None]
    return vals.transpose(0, 1, 3, 2).reshape(g * 512, n)


K, R, M, N, T, J = 512, 1024, 512, 512, 4096, 2048


def setup_inputs():
    n = np.random.standard_normal
    s = mx_kscale(K)[:, None]
    s2 = mx_kscale(K)[:, None]
    u = mx_kscale(R)[:, None]
    p_tab = pack_weight(n((K, T)) * s2, "e4m3")
    p_wk = pack_weight(n((K, R)) / np.sqrt(K) / s2 * u.T, "e2m1")
    return {
        "tab_words": p_tab[0],
        "tab_scales": p_tab[1],
        "x": (n((K, M)) * s).astype(np.float32),
        "wq": (n((K, R)) / np.sqrt(K) / s / u.T).astype(np.float32),
        "wk_words": p_wk[0],
        "wk_scales": p_wk[1],
        "offs": striped(np.random.permutation(T)[:J]),
    }


def reference(tab_words, tab_scales, x, wq, wk_words, wk_scales, offs):
    idx = unstriped(offs)
    tab_ = unpack_weight(tab_words, tab_scales, "e4m3")[:, idx]
    x_ = mxq(f64(x), 0, "e4m3")
    wq_ = mxq(f64(wq), 0, "e4m3")
    wk_ = unpack_weight(wk_words, wk_scales, "e2m1")
    qr = wq_.T @ x_
    kr = wk_.T @ tab_
    qr_ = mxq(qr, 0, "e4m3")
    kr_ = mxq(kr, 0, "e4m3")
    sc = qr_.T @ kr_
    return sc * 0.03125

@@ -1,0 +1,218 @@
+from contextlib import ExitStack
+
+import concourse.mybir as mybir
+
+K, R, M, T, J = 512, 1024, 512, 4096, 2048
+FLOPS = 2 * K * R * M + 2 * K * R * J + 2 * R * M * J
+
+F32 = mybir.dt.float32
+BF16 = mybir.dt.bfloat16
+I32 = mybir.dt.int32
+U32 = mybir.dt.uint32
+U16 = mybir.dt.uint16
+U8 = mybir.dt.uint8
+FP8X4 = mybir.dt.float8_e4m3fn_x4
+FP4X4 = mybir.dt.float4_e2m1fn_x4
+COPY = mybir.ActivationFunctionType.Copy
+MULT = mybir.AluOpType.mult
+
+P = 128
+PACK = 4
+PASS = P * PACK
+HALVES = R // PASS
+BANK = 512
+SUB = BANK // PACK
+GATHER = 512
+SCORE_SCALE = 0.03125
+GROUPS = [(0, 512), (512, 512), (1024, 512), (1536, 256), (1792, 256)]
+STEPS = [('sg', 1), ('rw', 1), ('rw', 0), ('perm',), ('qw', 0), ('x',), ('wg', 1), ('K', 1, 1, 3), ('sg', 0), ('wg', 0), ('K', 0, 0, 0), ('qx',), ('K', 1, 1, 0), ('Q', 0, 1), ('sg', 3), ('sg', 2), ('K', 0, 1, 0), ('qw', 1), ('K', 0, 0, 3), ('K', 1, 0, 3), ('K', 0, 1, 3), ('K', 0, 0, 1), ('K', 0, 1, 1), ('Q', 0, 3), ('Q', 1, 2), ('K', 1, 0, 0), ('K', 0, 1, 2), ('K', 0, 0, 2), ('K', 1, 0, 2), ('Q', 1, 0), ('Q', 0, 2), ('wg', 2), ('K', 2, 0, 2), ('qq', 0, '23'), ('K', 2, 1, 3), ('Q', 1, 1), ('Q', 1, 3), ('Q', 0, 0), ('qq', 1, '23'), ('qq', 1, '01'), ('K', 1, 1, 2), ('K', 1, 0, 1), ('K', 1, 1, 1), ('K', 2, 1, 2), ('qk', 0, 1), ('wg', 3), ('qk', 0, 0), ('S', 0, 2), ('K', 2, 0, 3), ('S', 0, 3), ('qk', 1, 0), ('qk', 1, 1), ('K', 3, 1, 1), ('K', 2, 1, 0), ('K', 4, 0, 0), ('qq', 0, '01'), ('K', 2, 1, 1), ('K', 3, 1, 0), ('K', 4, 0, 1), ('K', 2, 0, 1), ('K', 2, 0, 0), ('K', 3, 0, 0), ('S', 1, 2), ('S', 1, 3), ('K', 3, 0, 1), ('qk', 4, 0), ('qk', 2, 0), ('S', 1, 1), ('qk', 3, 1), ('S', 0, 1), ('K', 4, 1, 0), ('K', 4, 1, 1), ('qk', 3, 0), ('qk', 2, 1), ('S', 3, 0), ('S', 3, 1), ('S', 2, 2), ('S', 1, 0), ('qk', 4, 1), ('S', 2, 3), ('S', 4, 1), ('S', 0, 0), ('S', 2, 0), ('S', 2, 1), ('S', 4, 0)]
+ON_VECTOR = set([('K', 2, 0, 1), ('K', 3, 0, 0), ('K', 3, 1, 1), ('K', 4, 0, 1), ('Q', 0, 1), ('Q', 0, 3), ('Q', 1, 1), ('Q', 1, 2), ('S', 0, 0), ('S', 0, 2), ('S', 0, 3), ('S', 1, 0), ('S', 3, 0)])
+BANKS = [[0, 1, 2, 3], [4, 5, 6, 7]]
+RING = 2
+
+
+def tile_list_kvt_no_scale_kernel(
+    tc, tab_words, tab_scales, x, wq, wk_words, wk_scales, offs, out
+):
+    nc = tc.nc
+    with ExitStack() as ctx:
+        keep = ctx.enter_context(tc.tile_pool(name="keep", bufs=1))
+        psum = ctx.enter_context(tc.psum_pool(name="psum", bufs=1))
+
+        def tile(shape, dtype, name):
+            return keep.tile(shape, dtype, name=name, align_bytes=64)
+
+        offsets = keep.tile([P, J // 16], U16, name="offsets")
+        tab_w = tile([P, T], U32, "tab_w")
+        tab_s = tile([P, T], U8, "tab_s")
+        wk_raw_w = tile([P, R // 2], I32, "wk_raw_w")
+        wk_raw_s = tile([P, R // 4], I32, "wk_raw_s")
+        wk_w = tile([P, 2 * R], U8, "wk_w")
+        wk_s = tile([P, R], U8, "wk_s")
+        x_raw = tile([P, PACK, M], F32, "x_raw")
+        wq_raw = [tile([P, PACK, PASS], F32, "wq_raw%d" % h) for h in range(HALVES)]
+
+        nc.vector.memset(tab_s[:, : T // 2].bitcast(I32), 0)
+        nc.gpsimd.memset(tab_s[:, T // 2 :].bitcast(I32), 0)
+        nc.gpsimd.memset(wk_raw_s[:], 0)
+
+        nc.sync.dma_start(offsets[:], offs)
+        nc.sync.dma_start(wk_raw_w[:], wk_words[0].bitcast(I32))
+        for r in range(4):
+            nc.sync.dma_start(tab_s[r:P:32, :].bitcast(I32), tab_scales[0, r:16:4, :].bitcast(I32))
+        nc.sync.dma_start(tab_w[:].bitcast(I32), tab_words[0].rearrange("p t i -> p (t i)").bitcast(I32))
+        for r in range(4):
+            nc.gpsimd.dma_start(wk_raw_s[r:P:32, :], wk_scales[0, r:16:4, :].bitcast(I32))
+        nc.sync.dma_start(x_raw[:], x.rearrange("(p j) m -> p j m", j=PACK))
+        for h in range(HALVES):
+            nc.sync.dma_start(wq_raw[h][:], wq[:, h * PASS : (h + 1) * PASS].rearrange("(p j) r -> p j r", j=PACK))
+
+        got_w = [tile([P, GATHER], U32, "got_w%d" % c) for c in range(RING)]
+        got_s = [tile([P, GATHER], U8, "got_s%d" % c) for c in range(J // GATHER)]
+
+        def list_slice(c):
+            return offsets[:, c * GATHER // 16 : (c + 1) * GATHER // 16]
+
+        def gather_scales(c):
+            nc.vector.tensor_copy(got_s[c][:], tab_s[:].indirect(list_slice(c)))
+
+        def gather_words(c):
+            nc.vector.tensor_copy(got_w[c % RING][:], tab_w[:].indirect(list_slice(c)))
+
+        def permute_wk():
+            nc.vector.tensor_copy(
+                wk_w[:].bitcast(I32).rearrange("p (h t g w) -> p h t g w", h=HALVES, t=PACK, w=4),
+                wk_raw_w[:].rearrange("p (h g t w) -> p h t g w", h=HALVES, t=PACK, w=4),
+            )
+            nc.gpsimd.tensor_copy(
+                wk_s[:].bitcast(I32).rearrange("p (h t g w) -> p h t g w", h=HALVES, t=PACK, w=2),
+                wk_raw_s[:].rearrange("p (h g t w) -> p h t g w", h=HALVES, t=PACK, w=2),
+            )
+
+        def operand(width, name):
+            return (
+                tile([P, PACK * width], BF16, name + "_bf"),
+                tile([P, width], U32, name + "_w"),
+                tile([P, width], U8, name + "_s"),
+            )
+
+        def quantize(op, c0, c1):
+            nc.vector.quantize_mx(
+                out=op[1][:, c0:c1].bitcast(FP8X4), scales=op[2][:, c0:c1], in_=op[0][:, PACK * c0 : PACK * c1]
+            )
+
+        banks = [psum.tile([P, BANK], F32, name="bank%d" % b) for b in range(8)]
+        turns = {True: [], False: []}
+
+        def next_bank(on_vector):
+            key = on_vector and len(BANKS) == 2
+            mine = BANKS[1 if key else 0]
+            b = mine[len(turns[key]) % len(mine)]
+            turns[key].append(b)
+            return banks[b]
+
+        def project(step, lhs_of, rhs_w, rhs_s, dst):
+            on_vector = step in ON_VECTOR
+            acc = next_bank(on_vector)
+            for t in range(PACK):
+                lhs_w, lhs_s = lhs_of(t)
+                nc.tensor.matmul_mx(
+                    out=acc[:, t * SUB : (t + 1) * SUB], lhsT=lhs_w, lhsT_scale=lhs_s, rhs=rhs_w.bitcast(FP8X4),
+                    rhs_scale=rhs_s, start=True, stop=True,
+                )
+            dst = dst.rearrange("p (n t) -> p n t", t=PACK)
+            src = acc[:].rearrange("p (t n) -> p n t", t=PACK)
+            if on_vector:
+                nc.vector.tensor_copy(dst, src)
+            else:
+                nc.scalar.activation(dst, src, COPY)
+
+        x_op = operand(M, "x")
+        wq_op = [operand(PASS, "wq%d" % h) for h in range(HALVES)]
+        q_op = [operand(M, "q%d" % h) for h in range(HALVES)]
+        k_op = [[operand(w, "k%d_%d" % (g, h)) for h in range(HALVES)] for g, (j0, w) in enumerate(GROUPS)]
+
+        def round_x():
+            nc.vector.tensor_copy(
+                x_op[0][:].rearrange("p (c i j) -> p c j i", i=4, j=PACK),
+                x_raw[:].rearrange("p j (c i) -> p c j i", i=4),
+            )
+
+        def round_wq(h):
+            nc.vector.tensor_copy(
+                wq_op[h][0][:].rearrange("p (t g i j) -> p t g j i", t=PACK, i=8, j=PACK),
+                wq_raw[h][:].rearrange("p j (g t i) -> p t g j i", t=PACK, i=8),
+            )
+
+        def queries(step):
+            h, m0 = step[1], step[2] * SUB
+
+            def lhs_of(t):
+                cols = slice(t * P, (t + 1) * P)
+                return wq_op[h][1][:, cols].bitcast(FP8X4), wq_op[h][2][:, cols]
+
+            cols = slice(m0, m0 + SUB)
+            project(step, lhs_of, x_op[1][:, cols], x_op[2][:, cols], q_op[h][0][:, PACK * m0 : PACK * (m0 + SUB)])
+
+        def keys(step):
+            g, h, s0 = step[1], step[2], step[3] * SUB
+
+            def lhs_of(t):
+                r0 = h * PASS + t * P
+                return wk_w[:, 2 * r0 : 2 * (r0 + P)].bitcast(FP4X4), wk_s[:, r0 : r0 + P]
+
+            c, at = divmod(GROUPS[g][0] + s0, GATHER)
+            cols = slice(at, at + SUB)
+            project(step, lhs_of, got_w[c % RING][:, cols], got_s[c][:, cols], k_op[g][h][0][:, PACK * s0 : PACK * (s0 + SUB)])
+
+        out_v = out.rearrange("(a p) j -> p a j", p=P)
+
+        def scores(step):
+            g, b = step[1], step[2]
+            j0, w = GROUPS[g]
+            per_bank = BANK // w
+            on_vector = step in ON_VECTOR
+            acc = next_bank(on_vector)
+            for i in range(per_bank):
+                cols = slice((b * per_bank + i) * P, (b * per_bank + i + 1) * P)
+                for h in range(HALVES):
+                    nc.tensor.matmul_mx(
+                        out=acc[:, i * w : (i + 1) * w], lhsT=q_op[h][1][:, cols].bitcast(FP8X4),
+                        lhsT_scale=q_op[h][2][:, cols], rhs=k_op[g][h][1][:].bitcast(FP8X4), rhs_scale=k_op[g][h][2][:],
+                        start=(h == 0), stop=(h == HALVES - 1),
+                    )
+            res = tile([P, BANK], F32, "res%d_%d" % (g, b))
+            if on_vector:
+                nc.vector.tensor_scalar(res[:], acc[:], SCORE_SCALE, None, MULT)
+            else:
+                nc.scalar.activation(res[:], acc[:], COPY, scale=SCORE_SCALE)
+            nc.sync.dma_start(
+                out_v[:, b * per_bank : (b + 1) * per_bank, j0 : j0 + w], res[:].rearrange("p (a j) -> p a j", a=per_bank)
+            )
+
+        for step in STEPS:
+            kind = step[0]
+            if kind == "sg":
+                gather_scales(step[1])
+            elif kind == "wg":
+                gather_words(step[1])
+            elif kind == "perm":
+                permute_wk()
+            elif kind == "x":
+                round_x()
+            elif kind == "qx":
+                quantize(x_op, 0, M)
+            elif kind == "rw":
+                round_wq(step[1])
+            elif kind == "qw":
+                quantize(wq_op[step[1]], 0, PASS)
+            elif kind == "Q":
+                queries(step)
+            elif kind == "qq":
+                quantize(q_op[step[1]], int(step[2][0]) * P, (int(step[2][-1]) + 1) * P)
+            elif kind == "K":
+                keys(step)
+            elif kind == "qk":
+                quantize(k_op[step[1]][step[2]], 0, GROUPS[step[1]][1])
+            else:
+                scores(step)

@@ -25,9 +25,9 @@ SUB = BANK // PACK
 GATHER = 512
 SCORE_SCALE = 0.03125
 GROUPS = [(0, 512), (512, 512), (1024, 512), (1536, 256), (1792, 256)]
-STEPS = [('sg', 1), ('rw', 1), ('rw', 0), ('perm',), ('qw', 0), ('x',), ('wg', 1), ('K', 1, 1, 3), ('sg', 0), ('wg', 0), ('K', 0, 0, 0), ('qx',), ('K', 1, 1, 0), ('Q', 0, 1), ('sg', 3), ('sg', 2), ('K', 0, 1, 0), ('qw', 1), ('K', 0, 0, 3), ('K', 1, 0, 3), ('K', 0, 1, 3), ('K', 0, 0, 1), ('K', 0, 1, 1), ('Q', 0, 3), ('Q', 1, 2), ('K', 1, 0, 0), ('K', 0, 1, 2), ('K', 0, 0, 2), ('K', 1, 0, 2), ('Q', 1, 0), ('Q', 0, 2), ('wg', 2), ('K', 2, 0, 2), ('qq', 0, '23'), ('K', 2, 1, 3), ('Q', 1, 1), ('Q', 1, 3), ('Q', 0, 0), ('qq', 1, '23'), ('qq', 1, '01'), ('K', 1, 1, 2), ('K', 1, 0, 1), ('K', 1, 1, 1), ('K', 2, 1, 2), ('qk', 0, 1), ('wg', 3), ('qk', 0, 0), ('S', 0, 2), ('K', 2, 0, 3), ('S', 0, 3), ('qk', 1, 0), ('qk', 1, 1), ('K', 3, 1, 1), ('K', 2, 1, 0), ('K', 4, 0, 0), ('qq', 0, '01'), ('K', 2, 1, 1), ('K', 3, 1, 0), ('K', 4, 0, 1), ('K', 2, 0, 1), ('K', 2, 0, 0), ('K', 3, 0, 0), ('S', 1, 2), ('S', 1, 3), ('K', 3, 0, 1), ('qk', 4, 0), ('qk', 2, 0), ('S', 1, 1), ('qk', 3, 1), ('S', 0, 1), ('K', 4, 1, 0), ('K', 4, 1, 1), ('qk', 3, 0), ('qk', 2, 1), ('S', 3, 0), ('S', 3, 1), ('S', 2, 2), ('S', 1, 0), ('qk', 4, 1), ('S', 2, 3), ('S', 4, 1), ('S', 0, 0), ('S', 2, 0), ('S', 2, 1), ('S', 4, 0)]
-ON_VECTOR = set([('K', 2, 0, 1), ('K', 3, 0, 0), ('K', 3, 1, 1), ('K', 4, 0, 1), ('Q', 0, 1), ('Q', 0, 3), ('Q', 1, 1), ('Q', 1, 2), ('S', 0, 0), ('S', 0, 2), ('S', 0, 3), ('S', 1, 0), ('S', 3, 0)])
-BANKS = [[0, 1, 2, 3], [4, 5, 6, 7]]
+STEPS = [('perms',), ('wg', 0), ('x',), ('sg', 1), ('perm',), ('rw', 0), ('qw', 0), ('sg', 0), ('K', 0, 0, 0), ('qx',), ('Q', 0, 2), ('rw', 1), ('sg', 2), ('wg', 1), ('K', 0, 0, 1), ('K', 0, 0, 2), ('Q', 0, 0), ('K', 1, 0, 0), ('K', 0, 1, 0), ('K', 1, 0, 1), ('K', 0, 1, 1), ('Q', 0, 3), ('K', 0, 1, 2), ('qw', 1), ('Q', 0, 1), ('K', 0, 0, 3), ('qq', 0, '01'), ('K', 0, 1, 3), ('Q', 1, 1), ('K', 1, 0, 2), ('K', 1, 1, 0), ('wg', 2), ('K', 1, 0, 3), ('K', 1, 1, 1), ('Q', 1, 3), ('qq', 0, '23'), ('qk', 0, 1), ('K', 2, 0, 0), ('K', 1, 1, 2), ('K', 2, 0, 1), ('Q', 1, 2), ('qq', 1, '23'), ('sg', 3), ('Q', 1, 0), ('qk', 1, 0), ('qq', 1, '01'), ('qk', 0, 0), ('K', 2, 0, 2), ('K', 2, 1, 0), ('K', 1, 1, 3), ('K', 2, 0, 3), ('wg', 3), ('K', 2, 1, 1), ('S', 0, 1), ('K', 2, 1, 2), ('qk', 2, 0), ('qk', 1, 1), ('S', 1, 1), ('S', 0, 0), ('K', 2, 1, 3), ('S', 0, 2), ('K', 4, 0, 0), ('qk', 2, 1), ('K', 4, 1, 0), ('K', 3, 0, 0), ('K', 4, 1, 1), ('K', 3, 1, 0), ('S', 1, 2), ('S', 2, 1), ('K', 3, 1, 1), ('qk', 4, 1), ('S', 2, 0), ('S', 1, 3), ('K', 3, 0, 1), ('qk', 3, 0), ('S', 2, 2), ('K', 4, 0, 1), ('S', 0, 3), ('qk', 4, 0), ('S', 4, 1), ('S', 4, 0), ('S', 2, 3), ('qk', 3, 1), ('S', 3, 0), ('S', 3, 1), ('S', 1, 0)]
+ON_VECTOR = set([('K', 2, 1, 0), ('K', 2, 1, 3), ('K', 3, 0, 1), ('K', 4, 0, 0), ('K', 4, 1, 0), ('K', 4, 1, 1), ('Q', 0, 0), ('Q', 0, 1), ('Q', 1, 0), ('S', 0, 0), ('S', 0, 2), ('S', 1, 1), ('S', 1, 2), ('S', 2, 0), ('S', 2, 2), ('S', 2, 3)])
+BANKS = [[0, 1, 2, 3, 4, 5, 6, 7]]
 RING = 2
 
 
@@ -54,15 +54,15 @@ def tile_list_kvt_no_scale_kernel(
 
         nc.vector.memset(tab_s[:, : T // 2].bitcast(I32), 0)
         nc.gpsimd.memset(tab_s[:, T // 2 :].bitcast(I32), 0)
-        nc.gpsimd.memset(wk_raw_s[:], 0)
+        nc.vector.memset(wk_raw_s[:], 0)
 
         nc.sync.dma_start(offsets[:], offs)
         nc.sync.dma_start(wk_raw_w[:], wk_words[0].bitcast(I32))
         for r in range(4):
-            nc.sync.dma_start(tab_s[r:P:32, :].bitcast(I32), tab_scales[0, r:16:4, :].bitcast(I32))
+            (nc.sync if r < 2 else nc.scalar).dma_start(tab_s[r:P:32, :].bitcast(I32), tab_scales[0, r:16:4, :].bitcast(I32))
         nc.sync.dma_start(tab_w[:].bitcast(I32), tab_words[0].rearrange("p t i -> p (t i)").bitcast(I32))
         for r in range(4):
-            nc.gpsimd.dma_start(wk_raw_s[r:P:32, :], wk_scales[0, r:16:4, :].bitcast(I32))
+            nc.scalar.dma_start(wk_raw_s[r:P:32, :], wk_scales[0, r:16:4, :].bitcast(I32))
         nc.sync.dma_start(x_raw[:], x.rearrange("(p j) m -> p j m", j=PACK))
         for h in range(HALVES):
             nc.sync.dma_start(wq_raw[h][:], wq[:, h * PASS : (h + 1) * PASS].rearrange("(p j) r -> p j r", j=PACK))
@@ -84,7 +84,9 @@ def tile_list_kvt_no_scale_kernel(
                 wk_w[:].bitcast(I32).rearrange("p (h t g w) -> p h t g w", h=HALVES, t=PACK, w=4),
                 wk_raw_w[:].rearrange("p (h g t w) -> p h t g w", h=HALVES, t=PACK, w=4),
             )
-            nc.gpsimd.tensor_copy(
+
+        def permute_wk_scales():
+            nc.vector.tensor_copy(
                 wk_s[:].bitcast(I32).rearrange("p (h t g w) -> p h t g w", h=HALVES, t=PACK, w=2),
                 wk_raw_s[:].rearrange("p (h g t w) -> p h t g w", h=HALVES, t=PACK, w=2),
             )
@@ -198,6 +200,8 @@ def tile_list_kvt_no_scale_kernel(
                 gather_words(step[1])
             elif kind == "perm":
                 permute_wk()
+            elif kind == "perms":
+                permute_wk_scales()
             elif kind == "x":
                 round_x()
             elif kind == "qx":

@@ -25,8 +25,8 @@ SUB = BANK // PACK
 GATHER = 512
 SCORE_SCALE = 0.03125
 GROUPS = [(0, 512), (512, 512), (1024, 512), (1536, 256), (1792, 256)]
-STEPS = [('perms',), ('wg', 0), ('x',), ('sg', 1), ('perm',), ('rw', 0), ('qw', 0), ('sg', 0), ('K', 0, 0, 0), ('qx',), ('Q', 0, 2), ('rw', 1), ('sg', 2), ('wg', 1), ('K', 0, 0, 1), ('K', 0, 0, 2), ('Q', 0, 0), ('K', 1, 0, 0), ('K', 0, 1, 0), ('K', 1, 0, 1), ('K', 0, 1, 1), ('Q', 0, 3), ('K', 0, 1, 2), ('qw', 1), ('Q', 0, 1), ('K', 0, 0, 3), ('qq', 0, '01'), ('K', 0, 1, 3), ('Q', 1, 1), ('K', 1, 0, 2), ('K', 1, 1, 0), ('wg', 2), ('K', 1, 0, 3), ('K', 1, 1, 1), ('Q', 1, 3), ('qq', 0, '23'), ('qk', 0, 1), ('K', 2, 0, 0), ('K', 1, 1, 2), ('K', 2, 0, 1), ('Q', 1, 2), ('qq', 1, '23'), ('sg', 3), ('Q', 1, 0), ('qk', 1, 0), ('qq', 1, '01'), ('qk', 0, 0), ('K', 2, 0, 2), ('K', 2, 1, 0), ('K', 1, 1, 3), ('K', 2, 0, 3), ('wg', 3), ('K', 2, 1, 1), ('S', 0, 1), ('K', 2, 1, 2), ('qk', 2, 0), ('qk', 1, 1), ('S', 1, 1), ('S', 0, 0), ('K', 2, 1, 3), ('S', 0, 2), ('K', 4, 0, 0), ('qk', 2, 1), ('K', 4, 1, 0), ('K', 3, 0, 0), ('K', 4, 1, 1), ('K', 3, 1, 0), ('S', 1, 2), ('S', 2, 1), ('K', 3, 1, 1), ('qk', 4, 1), ('S', 2, 0), ('S', 1, 3), ('K', 3, 0, 1), ('qk', 3, 0), ('S', 2, 2), ('K', 4, 0, 1), ('S', 0, 3), ('qk', 4, 0), ('S', 4, 1), ('S', 4, 0), ('S', 2, 3), ('qk', 3, 1), ('S', 3, 0), ('S', 3, 1), ('S', 1, 0)]
-ON_VECTOR = set([('K', 2, 1, 0), ('K', 2, 1, 3), ('K', 3, 0, 1), ('K', 4, 0, 0), ('K', 4, 1, 0), ('K', 4, 1, 1), ('Q', 0, 0), ('Q', 0, 1), ('Q', 1, 0), ('S', 0, 0), ('S', 0, 2), ('S', 1, 1), ('S', 1, 2), ('S', 2, 0), ('S', 2, 2), ('S', 2, 3)])
+STEPS = [('sg', 0), ('wg', 0), ('perm',), ('perms',), ('K', 0, 1, 0), ('K', 0, 0, 0), ('K', 0, 1, 1), ('sg', 3), ('wg', 1), ('K', 0, 1, 2), ('K', 0, 0, 1), ('sg', 1), ('x',), ('sg', 2), ('rw', 0), ('K', 0, 0, 2), ('K', 1, 0, 0), ('K', 1, 0, 1), ('K', 1, 1, 0), ('K', 0, 1, 3), ('K', 1, 1, 1), ('K', 1, 1, 2), ('qw', 0), ('qx',), ('K', 1, 1, 3), ('K', 0, 0, 3), ('wg', 2), ('K', 1, 0, 2), ('rw', 1), ('qw', 1), ('Q', 0, 3), ('K', 2, 0, 0), ('Q', 0, 1), ('Q', 0, 0), ('qq', 0, '01'), ('K', 1, 0, 3), ('wg', 3), ('K', 2, 0, 1), ('K', 2, 0, 2), ('K', 2, 1, 0), ('Q', 0, 2), ('qk', 0, 0), ('qq', 0, '23'), ('K', 2, 1, 1), ('Q', 1, 3), ('K', 4, 0, 0), ('qk', 0, 1), ('qk', 1, 0), ('qk', 1, 1), ('K', 4, 1, 0), ('Q', 1, 2), ('Q', 1, 0), ('K', 4, 1, 1), ('K', 2, 1, 2), ('qk', 4, 1), ('K', 4, 0, 1), ('Q', 1, 1), ('qq', 1, '01'), ('K', 3, 0, 0), ('K', 2, 1, 3), ('qq', 1, '23'), ('qk', 4, 0), ('S', 4, 1), ('S', 0, 0), ('K', 3, 0, 1), ('S', 1, 2), ('S', 1, 3), ('S', 4, 0), ('qk', 2, 1), ('S', 1, 0), ('K', 2, 0, 3), ('K', 3, 1, 0), ('qk', 2, 0), ('S', 2, 0), ('S', 0, 1), ('S', 0, 2), ('S', 2, 2), ('S', 1, 1), ('S', 2, 3), ('K', 3, 1, 1), ('qk', 3, 1), ('S', 0, 3), ('qk', 3, 0), ('S', 3, 1), ('S', 3, 0), ('S', 2, 1)]
+ON_VECTOR = set([('K', 0, 1, 3), ('K', 1, 0, 0), ('K', 1, 0, 1), ('K', 2, 0, 0), ('K', 2, 0, 3), ('K', 3, 0, 1), ('K', 3, 1, 0), ('K', 3, 1, 1), ('Q', 1, 0), ('Q', 1, 2), ('S', 0, 2), ('S', 1, 1), ('S', 1, 2), ('S', 1, 3), ('S', 2, 0), ('S', 2, 1), ('S', 4, 1)])
 BANKS = [[0, 1, 2, 3, 4, 5, 6, 7]]
 RING = 2
 
@@ -46,7 +46,7 @@ def tile_list_kvt_no_scale_kernel(
         tab_w = tile([P, T], U32, "tab_w")
         tab_s = tile([P, T], U8, "tab_s")
         wk_raw_w = tile([P, R // 2], I32, "wk_raw_w")
-        wk_raw_s = tile([P, R // 4], I32, "wk_raw_s")
+        wk_raw_s = keep.tile([P, R // 4], I32, name="wk_raw_s", tag="shared", align_bytes=64)
         wk_w = tile([P, 2 * R], U8, "wk_w")
         wk_s = tile([P, R], U8, "wk_s")
         x_raw = tile([P, PACK, M], F32, "x_raw")
@@ -59,15 +59,15 @@ def tile_list_kvt_no_scale_kernel(
         nc.sync.dma_start(offsets[:], offs)
         nc.sync.dma_start(wk_raw_w[:], wk_words[0].bitcast(I32))
         for r in range(4):
-            (nc.sync if r < 2 else nc.scalar).dma_start(tab_s[r:P:32, :].bitcast(I32), tab_scales[0, r:16:4, :].bitcast(I32))
+            nc.sync.dma_start(tab_s[r:P:32, :].bitcast(I32), tab_scales[0, r:16:4, :].bitcast(I32))
         nc.sync.dma_start(tab_w[:].bitcast(I32), tab_words[0].rearrange("p t i -> p (t i)").bitcast(I32))
         for r in range(4):
-            nc.scalar.dma_start(wk_raw_s[r:P:32, :], wk_scales[0, r:16:4, :].bitcast(I32))
+            nc.sync.dma_start(wk_raw_s[r:P:32, :], wk_scales[0, r:16:4, :].bitcast(I32))
         nc.sync.dma_start(x_raw[:], x.rearrange("(p j) m -> p j m", j=PACK))
         for h in range(HALVES):
             nc.sync.dma_start(wq_raw[h][:], wq[:, h * PASS : (h + 1) * PASS].rearrange("(p j) r -> p j r", j=PACK))
 
-        got_w = [tile([P, GATHER], U32, "got_w%d" % c) for c in range(RING)]
+        got_w = [tile([P, GATHER], U32, "got_w0")]
         got_s = [tile([P, GATHER], U8, "got_s%d" % c) for c in range(J // GATHER)]
 
         def list_slice(c):
@@ -77,18 +77,20 @@ def tile_list_kvt_no_scale_kernel(
             nc.vector.tensor_copy(got_s[c][:], tab_s[:].indirect(list_slice(c)))
 
         def gather_words(c):
+            if c == 1:
+                got_w.append(keep.tile([P, GATHER], U32, name="got_w1", tag="shared", align_bytes=64))
             nc.vector.tensor_copy(got_w[c % RING][:], tab_w[:].indirect(list_slice(c)))
 
         def permute_wk():
             nc.vector.tensor_copy(
-                wk_w[:].bitcast(I32).rearrange("p (h t g w) -> p h t g w", h=HALVES, t=PACK, w=4),
-                wk_raw_w[:].rearrange("p (h g t w) -> p h t g w", h=HALVES, t=PACK, w=4),
+                wk_w[:].bitcast(I32).rearrange("p (h t g w) -> p h t g w", h=HALVES, t=PACK, w=2),
+                wk_raw_w[:].rearrange("p (h g t w) -> p h t g w", h=HALVES, t=PACK, w=2),
             )
 
         def permute_wk_scales():
             nc.vector.tensor_copy(
-                wk_s[:].bitcast(I32).rearrange("p (h t g w) -> p h t g w", h=HALVES, t=PACK, w=2),
-                wk_raw_s[:].rearrange("p (h g t w) -> p h t g w", h=HALVES, t=PACK, w=2),
+                wk_s[:].bitcast(I32).rearrange("p (h t g w) -> p h t g w", h=HALVES, t=PACK, w=1),
+                wk_raw_s[:].rearrange("p (h g t w) -> p h t g w", h=HALVES, t=PACK, w=1),
             )
 
         def operand(width, name):
@@ -142,8 +144,8 @@ def tile_list_kvt_no_scale_kernel(
 
         def round_wq(h):
             nc.vector.tensor_copy(
-                wq_op[h][0][:].rearrange("p (t g i j) -> p t g j i", t=PACK, i=8, j=PACK),
-                wq_raw[h][:].rearrange("p j (g t i) -> p t g j i", t=PACK, i=8),
+                wq_op[h][0][:].rearrange("p (t g i j) -> p t g j i", t=PACK, i=4, j=PACK),
+                wq_raw[h][:].rearrange("p j (g t i) -> p t g j i", t=PACK, i=4),
             )
 
         def queries(step):

@@ -25,9 +25,10 @@ SUB = BANK // PACK
 GATHER = 512
 SCORE_SCALE = 0.03125
 GROUPS = [(0, 512), (512, 512), (1024, 512), (1536, 256), (1792, 256)]
-STEPS = [('sg', 0), ('wg', 0), ('perm',), ('perms',), ('K', 0, 1, 0), ('K', 0, 0, 0), ('K', 0, 1, 1), ('sg', 3), ('wg', 1), ('K', 0, 1, 2), ('K', 0, 0, 1), ('sg', 1), ('x',), ('sg', 2), ('rw', 0), ('K', 0, 0, 2), ('K', 1, 0, 0), ('K', 1, 0, 1), ('K', 1, 1, 0), ('K', 0, 1, 3), ('K', 1, 1, 1), ('K', 1, 1, 2), ('qw', 0), ('qx',), ('K', 1, 1, 3), ('K', 0, 0, 3), ('wg', 2), ('K', 1, 0, 2), ('rw', 1), ('qw', 1), ('Q', 0, 3), ('K', 2, 0, 0), ('Q', 0, 1), ('Q', 0, 0), ('qq', 0, '01'), ('K', 1, 0, 3), ('wg', 3), ('K', 2, 0, 1), ('K', 2, 0, 2), ('K', 2, 1, 0), ('Q', 0, 2), ('qk', 0, 0), ('qq', 0, '23'), ('K', 2, 1, 1), ('Q', 1, 3), ('K', 4, 0, 0), ('qk', 0, 1), ('qk', 1, 0), ('qk', 1, 1), ('K', 4, 1, 0), ('Q', 1, 2), ('Q', 1, 0), ('K', 4, 1, 1), ('K', 2, 1, 2), ('qk', 4, 1), ('K', 4, 0, 1), ('Q', 1, 1), ('qq', 1, '01'), ('K', 3, 0, 0), ('K', 2, 1, 3), ('qq', 1, '23'), ('qk', 4, 0), ('S', 4, 1), ('S', 0, 0), ('K', 3, 0, 1), ('S', 1, 2), ('S', 1, 3), ('S', 4, 0), ('qk', 2, 1), ('S', 1, 0), ('K', 2, 0, 3), ('K', 3, 1, 0), ('qk', 2, 0), ('S', 2, 0), ('S', 0, 1), ('S', 0, 2), ('S', 2, 2), ('S', 1, 1), ('S', 2, 3), ('K', 3, 1, 1), ('qk', 3, 1), ('S', 0, 3), ('qk', 3, 0), ('S', 3, 1), ('S', 3, 0), ('S', 2, 1)]
-ON_VECTOR = set([('K', 0, 1, 3), ('K', 1, 0, 0), ('K', 1, 0, 1), ('K', 2, 0, 0), ('K', 2, 0, 3), ('K', 3, 0, 1), ('K', 3, 1, 0), ('K', 3, 1, 1), ('Q', 1, 0), ('Q', 1, 2), ('S', 0, 2), ('S', 1, 1), ('S', 1, 2), ('S', 1, 3), ('S', 2, 0), ('S', 2, 1), ('S', 4, 1)])
-BANKS = [[0, 1, 2, 3, 4, 5, 6, 7]]
+STEPS = [('sg', 2), ('perms',), ('sg', 0), ('wg', 0), ('perm',), ('wg', 1), ('K', 0, 0, 0), ('sg', 1), ('K', 0, 1, 0), ('K', 0, 0, 1), ('K', 1, 0, 0), ('K', 0, 1, 1), ('rw', 1), ('K', 0, 0, 2), ('K', 0, 1, 2), ('x',), ('K', 1, 1, 0), ('rw', 0), ('K', 1, 1, 1), ('K', 1, 0, 1), ('K', 1, 0, 2), ('K', 0, 1, 3), ('K', 1, 1, 2), ('K', 0, 0, 3), ('qw', 1), ('qx',), ('qw', 0), ('wg', 2), ('K', 1, 0, 3), ('qk', 1, 0), ('Q', 0, 1), ('K', 1, 1, 3), ('qk', 0, 0), ('qk', 1, 1), ('K', 2, 0, 0), ('Q', 0, 0), ('Q', 1, 1), ('Q', 1, 0), ('Q', 0, 2), ('K', 2, 0, 1), ('K', 2, 1, 0), ('K', 2, 0, 2), ('Q', 0, 3), ('qq', 0, '01'), ('Q', 1, 2), ('K', 2, 0, 3), ('sg', 3), ('qq', 1, '01'), ('S', 1, 1), ('wg', 3), ('Q', 1, 3), ('K', 3, 1, 0), ('qq', 1, '23'), ('qq', 0, '23'), ('K', 2, 1, 1), ('qk', 0, 1), ('S', 0, 1), ('K', 4, 1, 0), ('S', 1, 0), ('K', 2, 1, 2), ('K', 2, 1, 3), ('qk', 2, 0), ('S', 1, 3), ('qk', 2, 1), ('S', 0, 3), ('S', 0, 2), ('S', 2, 2), ('K', 3, 0, 0), ('S', 0, 0), ('K', 3, 0, 1), ('qk', 3, 0), ('K', 3, 1, 1), ('S', 2, 0), ('S', 1, 2), ('qk', 3, 1), ('K', 4, 0, 0), ('K', 4, 0, 1), ('qk', 4, 0), ('S', 2, 3), ('K', 4, 1, 1), ('qk', 4, 1), ('S', 4, 1), ('S', 3, 1), ('S', 4, 0), ('S', 2, 1), ('S', 3, 0)]
+ON_VECTOR = set([('K', 2, 1, 2), ('K', 2, 1, 3), ('K', 3, 0, 1), ('K', 4, 0, 0), ('K', 4, 0, 1), ('K', 4, 1, 0), ('K', 4, 1, 1), ('Q', 0, 0), ('Q', 1, 0), ('Q', 1, 3), ('S', 0, 0), ('S', 1, 0), ('S', 4, 0)])
+BANKS = [[0, 1, 2, 3], [4, 5, 6, 7]]
+FIRST_KEYS = ("K", 0, 0, 0)
 RING = 2
 
 
@@ -128,8 +129,10 @@ def tile_list_kvt_no_scale_kernel(
             src = acc[:].rearrange("p (t n) -> p n t", t=PACK)
             if on_vector:
                 nc.vector.tensor_copy(dst, src)
-            else:
+            elif step == FIRST_KEYS:
                 nc.scalar.activation(dst, src, COPY)
+            else:
+                nc.scalar.copy(dst, src)
 
         x_op = operand(M, "x")
         wq_op = [operand(PASS, "wq%d" % h) for h in range(HALVES)]

@@ -20,16 +20,44 @@ P = 128
 PACK = 4
 PASS = P * PACK
 HALVES = R // PASS
+RUN = 4
+QUADRANT = 32
+SCALE_ROWS = 4
+BLOCKS = PASS // 32
 BANK = 512
-SUB = BANK // PACK
-GATHER = 512
+BLOCK = BANK // PACK
+SLICE = 512
+OFFSETS_PER_COLUMN = 16
+WORD_TILES = 2
 SCORE_SCALE = 0.03125
+
 GROUPS = [(0, 512), (512, 512), (1024, 512), (1536, 256), (1792, 256)]
-STEPS = [('sg', 2), ('perms',), ('sg', 0), ('wg', 0), ('perm',), ('wg', 1), ('K', 0, 0, 0), ('sg', 1), ('K', 0, 1, 0), ('K', 0, 0, 1), ('K', 1, 0, 0), ('K', 0, 1, 1), ('rw', 1), ('K', 0, 0, 2), ('K', 0, 1, 2), ('x',), ('K', 1, 1, 0), ('rw', 0), ('K', 1, 1, 1), ('K', 1, 0, 1), ('K', 1, 0, 2), ('K', 0, 1, 3), ('K', 1, 1, 2), ('K', 0, 0, 3), ('qw', 1), ('qx',), ('qw', 0), ('wg', 2), ('K', 1, 0, 3), ('qk', 1, 0), ('Q', 0, 1), ('K', 1, 1, 3), ('qk', 0, 0), ('qk', 1, 1), ('K', 2, 0, 0), ('Q', 0, 0), ('Q', 1, 1), ('Q', 1, 0), ('Q', 0, 2), ('K', 2, 0, 1), ('K', 2, 1, 0), ('K', 2, 0, 2), ('Q', 0, 3), ('qq', 0, '01'), ('Q', 1, 2), ('K', 2, 0, 3), ('sg', 3), ('qq', 1, '01'), ('S', 1, 1), ('wg', 3), ('Q', 1, 3), ('K', 3, 1, 0), ('qq', 1, '23'), ('qq', 0, '23'), ('K', 2, 1, 1), ('qk', 0, 1), ('S', 0, 1), ('K', 4, 1, 0), ('S', 1, 0), ('K', 2, 1, 2), ('K', 2, 1, 3), ('qk', 2, 0), ('S', 1, 3), ('qk', 2, 1), ('S', 0, 3), ('S', 0, 2), ('S', 2, 2), ('K', 3, 0, 0), ('S', 0, 0), ('K', 3, 0, 1), ('qk', 3, 0), ('K', 3, 1, 1), ('S', 2, 0), ('S', 1, 2), ('qk', 3, 1), ('K', 4, 0, 0), ('K', 4, 0, 1), ('qk', 4, 0), ('S', 2, 3), ('K', 4, 1, 1), ('qk', 4, 1), ('S', 4, 1), ('S', 3, 1), ('S', 4, 0), ('S', 2, 1), ('S', 3, 0)]
-ON_VECTOR = set([('K', 2, 1, 2), ('K', 2, 1, 3), ('K', 3, 0, 1), ('K', 4, 0, 0), ('K', 4, 0, 1), ('K', 4, 1, 0), ('K', 4, 1, 1), ('Q', 0, 0), ('Q', 1, 0), ('Q', 1, 3), ('S', 0, 0), ('S', 1, 0), ('S', 4, 0)])
-BANKS = [[0, 1, 2, 3], [4, 5, 6, 7]]
-FIRST_KEYS = ("K", 0, 0, 0)
-RING = 2
+
+S, V = "scalar", "vector"
+BANKS_OF = {S: (0, 1, 2, 3), V: (4, 5, 6, 7)}
+
+ORDER = [
+    ("order wk words",), ("gather scales", 0), ("gather scales", 1), ("gather scales", 2), ("gather scales", 3),
+    ("gather words", 0), ("order wk scales",), ("gather words", 1),
+    ("keys", 0, 0, 0, S), ("round x",), ("keys", 0, 0, 1, S), ("keys", 0, 0, 2, S), ("keys", 0, 1, 0, S),
+    ("quantise x",), ("keys", 0, 1, 1, S), ("round wq", 0), ("keys", 0, 1, 2, S), ("keys", 0, 0, 3, S),
+    ("keys", 1, 0, 0, S), ("keys", 1, 0, 1, S), ("round wq", 1), ("keys", 0, 1, 3, S), ("keys", 1, 0, 2, S),
+    ("quantise wq", 0), ("keys", 1, 0, 3, S), ("quantise wq", 1), ("keys", 1, 1, 0, S), ("keys", 1, 1, 1, S),
+    ("gather words", 2), ("keys", 1, 1, 2, S),
+    ("quantise k", 0, 0), ("queries", 0, 0, S), ("keys", 1, 1, 3, S), ("quantise k", 1, 0), ("quantise k", 1, 1),
+    ("keys", 2, 0, 0, S), ("queries", 1, 0, S), ("queries", 0, 1, V), ("queries", 0, 2, V), ("queries", 1, 1, S),
+    ("keys", 2, 0, 1, S), ("quantise q", 0, 0), ("quantise q", 1, 0), ("keys", 2, 0, 2, S), ("gather words", 3),
+    ("keys", 2, 0, 3, S), ("queries", 0, 3, S), ("queries", 1, 2, V), ("queries", 1, 3, S), ("quantise q", 0, 1),
+    ("keys", 2, 1, 0, S), ("quantise q", 1, 1), ("quantise k", 0, 1),
+    ("scores", 1, 0, S), ("keys", 2, 1, 1, S), ("keys", 2, 1, 2, V), ("keys", 2, 1, 3, S), ("scores", 0, 0, S),
+    ("scores", 1, 1, V), ("keys", 3, 0, 0, V), ("scores", 0, 1, S), ("keys", 3, 0, 1, V), ("quantise k", 2, 0),
+    ("scores", 0, 2, S), ("quantise k", 2, 1), ("scores", 0, 3, S), ("scores", 1, 2, S), ("keys", 3, 1, 0, S),
+    ("scores", 1, 3, V), ("keys", 3, 1, 1, V), ("keys", 4, 0, 0, S), ("quantise k", 3, 0), ("quantise k", 3, 1),
+    ("keys", 4, 0, 1, V), ("scores", 2, 0, S), ("keys", 4, 1, 0, V), ("scores", 2, 1, S), ("scores", 2, 2, S),
+    ("quantise k", 4, 0), ("keys", 4, 1, 1, V), ("quantise k", 4, 1), ("scores", 2, 3, S), ("scores", 3, 0, S),
+    ("scores", 3, 1, S), ("scores", 4, 0, S), ("scores", 4, 1, V),
+]
+FIRST_KEYS = (0, 0, 0)
 
 
 def tile_list_kvt_no_scale_kernel(
@@ -43,7 +71,7 @@ def tile_list_kvt_no_scale_kernel(
         def tile(shape, dtype, name):
             return keep.tile(shape, dtype, name=name, align_bytes=64)
 
-        offsets = keep.tile([P, J // 16], U16, name="offsets")
+        offsets = keep.tile([P, J // OFFSETS_PER_COLUMN], U16, name="offsets")
         tab_w = tile([P, T], U32, "tab_w")
         tab_s = tile([P, T], U8, "tab_s")
         wk_raw_w = tile([P, R // 2], I32, "wk_raw_w")
@@ -59,40 +87,20 @@ def tile_list_kvt_no_scale_kernel(
 
         nc.sync.dma_start(offsets[:], offs)
         nc.sync.dma_start(wk_raw_w[:], wk_words[0].bitcast(I32))
-        for r in range(4):
-            nc.sync.dma_start(tab_s[r:P:32, :].bitcast(I32), tab_scales[0, r:16:4, :].bitcast(I32))
+        for row in range(SCALE_ROWS):
+            nc.sync.dma_start(tab_s[row:P:QUADRANT, :].bitcast(I32), tab_scales[0, row:BLOCKS:SCALE_ROWS, :].bitcast(I32))
         nc.sync.dma_start(tab_w[:].bitcast(I32), tab_words[0].rearrange("p t i -> p (t i)").bitcast(I32))
-        for r in range(4):
-            nc.sync.dma_start(wk_raw_s[r:P:32, :], wk_scales[0, r:16:4, :].bitcast(I32))
-        nc.sync.dma_start(x_raw[:], x.rearrange("(p j) m -> p j m", j=PACK))
+        for row in range(SCALE_ROWS):
+            nc.sync.dma_start(wk_raw_s[row:P:QUADRANT, :], wk_scales[0, row:BLOCKS:SCALE_ROWS, :].bitcast(I32))
+        nc.sync.dma_start(x_raw[:], x.rearrange("(p code) m -> p code m", code=PACK))
         for h in range(HALVES):
-            nc.sync.dma_start(wq_raw[h][:], wq[:, h * PASS : (h + 1) * PASS].rearrange("(p j) r -> p j r", j=PACK))
+            rows = wq[:, h * PASS : (h + 1) * PASS]
+            nc.sync.dma_start(wq_raw[h][:], rows.rearrange("(p code) r -> p code r", code=PACK))
 
-        got_w = [tile([P, GATHER], U32, "got_w0")]
-        got_s = [tile([P, GATHER], U8, "got_s%d" % c) for c in range(J // GATHER)]
-
-        def list_slice(c):
-            return offsets[:, c * GATHER // 16 : (c + 1) * GATHER // 16]
-
-        def gather_scales(c):
-            nc.vector.tensor_copy(got_s[c][:], tab_s[:].indirect(list_slice(c)))
-
-        def gather_words(c):
-            if c == 1:
-                got_w.append(keep.tile([P, GATHER], U32, name="got_w1", tag="shared", align_bytes=64))
-            nc.vector.tensor_copy(got_w[c % RING][:], tab_w[:].indirect(list_slice(c)))
-
-        def permute_wk():
-            nc.vector.tensor_copy(
-                wk_w[:].bitcast(I32).rearrange("p (h t g w) -> p h t g w", h=HALVES, t=PACK, w=2),
-                wk_raw_w[:].rearrange("p (h g t w) -> p h t g w", h=HALVES, t=PACK, w=2),
-            )
-
-        def permute_wk_scales():
-            nc.vector.tensor_copy(
-                wk_s[:].bitcast(I32).rearrange("p (h t g w) -> p h t g w", h=HALVES, t=PACK, w=1),
-                wk_raw_s[:].rearrange("p (h g t w) -> p h t g w", h=HALVES, t=PACK, w=1),
-            )
+        got_w = [tile([P, SLICE], U32, "got_w0")]
+        got_s = [tile([P, SLICE], U8, "got_s%d" % n) for n in range(J // SLICE)]
+        banks = [psum.tile([P, BANK], F32, name="bank%d" % b) for b in range(8)]
+        banks_taken = {S: 0, V: 0}
 
         def operand(width, name):
             return (
@@ -101,127 +109,127 @@ def tile_list_kvt_no_scale_kernel(
                 tile([P, width], U8, name + "_s"),
             )
 
-        def quantize(op, c0, c1):
-            nc.vector.quantize_mx(
-                out=op[1][:, c0:c1].bitcast(FP8X4), scales=op[2][:, c0:c1], in_=op[0][:, PACK * c0 : PACK * c1]
-            )
-
-        banks = [psum.tile([P, BANK], F32, name="bank%d" % b) for b in range(8)]
-        turns = {True: [], False: []}
-
-        def next_bank(on_vector):
-            key = on_vector and len(BANKS) == 2
-            mine = BANKS[1 if key else 0]
-            b = mine[len(turns[key]) % len(mine)]
-            turns[key].append(b)
-            return banks[b]
-
-        def project(step, lhs_of, rhs_w, rhs_s, dst):
-            on_vector = step in ON_VECTOR
-            acc = next_bank(on_vector)
-            for t in range(PACK):
-                lhs_w, lhs_s = lhs_of(t)
-                nc.tensor.matmul_mx(
-                    out=acc[:, t * SUB : (t + 1) * SUB], lhsT=lhs_w, lhsT_scale=lhs_s, rhs=rhs_w.bitcast(FP8X4),
-                    rhs_scale=rhs_s, start=True, stop=True,
-                )
-            dst = dst.rearrange("p (n t) -> p n t", t=PACK)
-            src = acc[:].rearrange("p (t n) -> p n t", t=PACK)
-            if on_vector:
-                nc.vector.tensor_copy(dst, src)
-            elif step == FIRST_KEYS:
-                nc.scalar.activation(dst, src, COPY)
-            else:
-                nc.scalar.copy(dst, src)
-
         x_op = operand(M, "x")
         wq_op = [operand(PASS, "wq%d" % h) for h in range(HALVES)]
         q_op = [operand(M, "q%d" % h) for h in range(HALVES)]
-        k_op = [[operand(w, "k%d_%d" % (g, h)) for h in range(HALVES)] for g, (j0, w) in enumerate(GROUPS)]
+        k_op = [[operand(width, "k%d_%d" % (g, h)) for h in range(HALVES)] for g, (j0, width) in enumerate(GROUPS)]
+        out_tiles = out.rearrange("(a p) j -> p a j", p=P)
+
+        def list_slice(n):
+            columns = SLICE // OFFSETS_PER_COLUMN
+            return offsets[:, n * columns : (n + 1) * columns]
+
+        def gather_scales(n):
+            nc.vector.tensor_copy(got_s[n][:], tab_s[:].indirect(list_slice(n)))
+
+        def gather_words(n):
+            if n == WORD_TILES - 1:
+                got_w.append(keep.tile([P, SLICE], U32, name="got_w1", tag="shared", align_bytes=64))
+            nc.vector.tensor_copy(got_w[n % WORD_TILES][:], tab_w[:].indirect(list_slice(n)))
+
+        def order_columns(ordered, raw, elements_per_run):
+            nc.vector.tensor_copy(
+                ordered[:].bitcast(I32).rearrange("p (h t c e) -> p h t c e", h=HALVES, t=PACK, e=elements_per_run),
+                raw[:].rearrange("p (h c t e) -> p h t c e", h=HALVES, t=PACK, e=elements_per_run),
+            )
 
         def round_x():
             nc.vector.tensor_copy(
-                x_op[0][:].rearrange("p (c i j) -> p c j i", i=4, j=PACK),
-                x_raw[:].rearrange("p j (c i) -> p c j i", i=4),
+                x_op[0][:].rearrange("p (c i code) -> p c code i", i=RUN, code=PACK),
+                x_raw[:].rearrange("p code (c i) -> p c code i", i=RUN),
             )
 
         def round_wq(h):
             nc.vector.tensor_copy(
-                wq_op[h][0][:].rearrange("p (t g i j) -> p t g j i", t=PACK, i=4, j=PACK),
-                wq_raw[h][:].rearrange("p j (g t i) -> p t g j i", t=PACK, i=4),
+                wq_op[h][0][:].rearrange("p (t c i code) -> p t c code i", t=PACK, i=RUN, code=PACK),
+                wq_raw[h][:].rearrange("p code (c t i) -> p t c code i", t=PACK, i=RUN),
             )
 
-        def queries(step):
-            h, m0 = step[1], step[2] * SUB
+        def quantise(op, first, width):
+            values, words, scales = op
+            nc.vector.quantize_mx(
+                out=words[:, first : first + width].bitcast(FP8X4),
+                scales=scales[:, first : first + width],
+                in_=values[:, PACK * first : PACK * (first + width)],
+            )
 
-            def lhs_of(t):
-                cols = slice(t * P, (t + 1) * P)
-                return wq_op[h][1][:, cols].bitcast(FP8X4), wq_op[h][2][:, cols]
+        def take_bank(engine):
+            own = BANKS_OF[engine]
+            bank = banks[own[banks_taken[engine] % len(own)]]
+            banks_taken[engine] += 1
+            return bank
 
-            cols = slice(m0, m0 + SUB)
-            project(step, lhs_of, x_op[1][:, cols], x_op[2][:, cols], q_op[h][0][:, PACK * m0 : PACK * (m0 + SUB)])
+        def project(weights, moving_w, moving_s, values, engine, as_activation):
+            bank = take_bank(engine)
+            for t in range(PACK):
+                nc.tensor.matmul_mx(
+                    out=bank[:, t * BLOCK : (t + 1) * BLOCK], lhsT=weights[t][0], lhsT_scale=weights[t][1],
+                    rhs=moving_w.bitcast(FP8X4), rhs_scale=moving_s, start=True, stop=True,
+                )
+            dst = values.rearrange("p (n t) -> p n t", t=PACK)
+            src = bank[:].rearrange("p (t n) -> p n t", t=PACK)
+            if engine == V:
+                nc.vector.tensor_copy(dst, src)
+            elif as_activation:
+                nc.scalar.activation(dst, src, COPY)
+            else:
+                nc.scalar.copy(dst, src)
 
-        def keys(step):
-            g, h, s0 = step[1], step[2], step[3] * SUB
+        def queries(h, block, engine):
+            weights = [
+                (wq_op[h][1][:, t * P : (t + 1) * P].bitcast(FP8X4), wq_op[h][2][:, t * P : (t + 1) * P])
+                for t in range(PACK)
+            ]
+            cols = slice(block * BLOCK, (block + 1) * BLOCK)
+            values = q_op[h][0][:, PACK * cols.start : PACK * cols.stop]
+            project(weights, x_op[1][:, cols], x_op[2][:, cols], values, engine, False)
 
-            def lhs_of(t):
-                r0 = h * PASS + t * P
-                return wk_w[:, 2 * r0 : 2 * (r0 + P)].bitcast(FP4X4), wk_s[:, r0 : r0 + P]
+        def keys(g, h, block, engine):
+            firsts = [h * PASS + t * P for t in range(PACK)]
+            weights = [(wk_w[:, 2 * r0 : 2 * (r0 + P)].bitcast(FP4X4), wk_s[:, r0 : r0 + P]) for r0 in firsts]
+            n, at = divmod(GROUPS[g][0] + block * BLOCK, SLICE)
+            cols = slice(at, at + BLOCK)
+            values = k_op[g][h][0][:, PACK * block * BLOCK : PACK * (block + 1) * BLOCK]
+            as_activation = (g, h, block) == FIRST_KEYS
+            project(weights, got_w[n % WORD_TILES][:, cols], got_s[n][:, cols], values, engine, as_activation)
 
-            c, at = divmod(GROUPS[g][0] + s0, GATHER)
-            cols = slice(at, at + SUB)
-            project(step, lhs_of, got_w[c % RING][:, cols], got_s[c][:, cols], k_op[g][h][0][:, PACK * s0 : PACK * (s0 + SUB)])
-
-        out_v = out.rearrange("(a p) j -> p a j", p=P)
-
-        def scores(step):
-            g, b = step[1], step[2]
-            j0, w = GROUPS[g]
-            per_bank = BANK // w
-            on_vector = step in ON_VECTOR
-            acc = next_bank(on_vector)
-            for i in range(per_bank):
-                cols = slice((b * per_bank + i) * P, (b * per_bank + i + 1) * P)
+        def scores(g, b, engine):
+            j0, width = GROUPS[g]
+            per_bank = BANK // width
+            bank = take_bank(engine)
+            for slot in range(per_bank):
+                rows = slice((b * per_bank + slot) * P, (b * per_bank + slot + 1) * P)
                 for h in range(HALVES):
                     nc.tensor.matmul_mx(
-                        out=acc[:, i * w : (i + 1) * w], lhsT=q_op[h][1][:, cols].bitcast(FP8X4),
-                        lhsT_scale=q_op[h][2][:, cols], rhs=k_op[g][h][1][:].bitcast(FP8X4), rhs_scale=k_op[g][h][2][:],
+                        out=bank[:, slot * width : (slot + 1) * width],
+                        lhsT=q_op[h][1][:, rows].bitcast(FP8X4), lhsT_scale=q_op[h][2][:, rows],
+                        rhs=k_op[g][h][1][:].bitcast(FP8X4), rhs_scale=k_op[g][h][2][:],
                         start=(h == 0), stop=(h == HALVES - 1),
                     )
-            res = tile([P, BANK], F32, "res%d_%d" % (g, b))
-            if on_vector:
-                nc.vector.tensor_scalar(res[:], acc[:], SCORE_SCALE, None, MULT)
+            result = tile([P, BANK], F32, "res%d_%d" % (g, b))
+            if engine == V:
+                nc.vector.tensor_scalar(result[:], bank[:], SCORE_SCALE, None, MULT)
             else:
-                nc.scalar.activation(res[:], acc[:], COPY, scale=SCORE_SCALE)
+                nc.scalar.activation(result[:], bank[:], COPY, scale=SCORE_SCALE)
             nc.sync.dma_start(
-                out_v[:, b * per_bank : (b + 1) * per_bank, j0 : j0 + w], res[:].rearrange("p (a j) -> p a j", a=per_bank)
+                out_tiles[:, b * per_bank : (b + 1) * per_bank, j0 : j0 + width],
+                result[:].rearrange("p (a j) -> p a j", a=per_bank),
             )
 
-        for step in STEPS:
-            kind = step[0]
-            if kind == "sg":
-                gather_scales(step[1])
-            elif kind == "wg":
-                gather_words(step[1])
-            elif kind == "perm":
-                permute_wk()
-            elif kind == "perms":
-                permute_wk_scales()
-            elif kind == "x":
-                round_x()
-            elif kind == "qx":
-                quantize(x_op, 0, M)
-            elif kind == "rw":
-                round_wq(step[1])
-            elif kind == "qw":
-                quantize(wq_op[step[1]], 0, PASS)
-            elif kind == "Q":
-                queries(step)
-            elif kind == "qq":
-                quantize(q_op[step[1]], int(step[2][0]) * P, (int(step[2][-1]) + 1) * P)
-            elif kind == "K":
-                keys(step)
-            elif kind == "qk":
-                quantize(k_op[step[1]][step[2]], 0, GROUPS[step[1]][1])
-            else:
-                scores(step)
+        steps = {
+            "order wk words": lambda: order_columns(wk_w, wk_raw_w, 2),
+            "order wk scales": lambda: order_columns(wk_s, wk_raw_s, 1),
+            "gather scales": gather_scales,
+            "gather words": gather_words,
+            "round x": round_x,
+            "round wq": round_wq,
+            "quantise x": lambda: quantise(x_op, 0, M),
+            "quantise wq": lambda h: quantise(wq_op[h], 0, PASS),
+            "quantise q": lambda h, half: quantise(q_op[h], half * M // 2, M // 2),
+            "quantise k": lambda g, h: quantise(k_op[g][h], 0, GROUPS[g][1]),
+            "queries": queries,
+            "keys": keys,
+            "scores": scores,
+        }
+        for step in ORDER:
+            steps[step[0]](*step[1:])

@@ -25,39 +25,16 @@ QUADRANT = 32
 SCALE_ROWS = 4
 BLOCKS = PASS // 32
 BANK = 512
+BANKS = 8
 BLOCK = BANK // PACK
+GROUP = 256
 SLICE = 512
 OFFSETS_PER_COLUMN = 16
-WORD_TILES = 2
 SCORE_SCALE = 0.03125
-
-GROUPS = [(0, 512), (512, 512), (1024, 512), (1536, 256), (1792, 256)]
-
-S, V = "scalar", "vector"
-BANKS_OF = {S: (0, 1, 2, 3), V: (4, 5, 6, 7)}
-
-ORDER = [
-    ("order wk words",), ("gather scales", 0), ("gather scales", 1), ("gather scales", 2), ("gather scales", 3),
-    ("gather words", 0), ("order wk scales",), ("gather words", 1),
-    ("keys", 0, 0, 0, S), ("round x",), ("keys", 0, 0, 1, S), ("keys", 0, 0, 2, S), ("keys", 0, 1, 0, S),
-    ("quantise x",), ("keys", 0, 1, 1, S), ("round wq", 0), ("keys", 0, 1, 2, S), ("keys", 0, 0, 3, S),
-    ("keys", 1, 0, 0, S), ("keys", 1, 0, 1, S), ("round wq", 1), ("keys", 0, 1, 3, S), ("keys", 1, 0, 2, S),
-    ("quantise wq", 0), ("keys", 1, 0, 3, S), ("quantise wq", 1), ("keys", 1, 1, 0, S), ("keys", 1, 1, 1, S),
-    ("gather words", 2), ("keys", 1, 1, 2, S),
-    ("quantise k", 0, 0), ("queries", 0, 0, S), ("keys", 1, 1, 3, S), ("quantise k", 1, 0), ("quantise k", 1, 1),
-    ("keys", 2, 0, 0, S), ("queries", 1, 0, S), ("queries", 0, 1, V), ("queries", 0, 2, V), ("queries", 1, 1, S),
-    ("keys", 2, 0, 1, S), ("quantise q", 0, 0), ("quantise q", 1, 0), ("keys", 2, 0, 2, S), ("gather words", 3),
-    ("keys", 2, 0, 3, S), ("queries", 0, 3, S), ("queries", 1, 2, V), ("queries", 1, 3, S), ("quantise q", 0, 1),
-    ("keys", 2, 1, 0, S), ("quantise q", 1, 1), ("quantise k", 0, 1),
-    ("scores", 1, 0, S), ("keys", 2, 1, 1, S), ("keys", 2, 1, 2, V), ("keys", 2, 1, 3, S), ("scores", 0, 0, S),
-    ("scores", 1, 1, V), ("keys", 3, 0, 0, V), ("scores", 0, 1, S), ("keys", 3, 0, 1, V), ("quantise k", 2, 0),
-    ("scores", 0, 2, S), ("quantise k", 2, 1), ("scores", 0, 3, S), ("scores", 1, 2, S), ("keys", 3, 1, 0, S),
-    ("scores", 1, 3, V), ("keys", 3, 1, 1, V), ("keys", 4, 0, 0, S), ("quantise k", 3, 0), ("quantise k", 3, 1),
-    ("keys", 4, 0, 1, V), ("scores", 2, 0, S), ("keys", 4, 1, 0, V), ("scores", 2, 1, S), ("scores", 2, 2, S),
-    ("quantise k", 4, 0), ("keys", 4, 1, 1, V), ("quantise k", 4, 1), ("scores", 2, 3, S), ("scores", 3, 0, S),
-    ("scores", 3, 1, S), ("scores", 4, 0, S), ("scores", 4, 1, V),
-]
-FIRST_KEYS = (0, 0, 0)
+VECTOR_FROM = 14
+VECTOR_EVERY = 4
+QUERIES_AT = (10,11)
+SCORES_FROM = 19
 
 
 def tile_list_kvt_no_scale_kernel(
@@ -68,22 +45,30 @@ def tile_list_kvt_no_scale_kernel(
         keep = ctx.enter_context(tc.tile_pool(name="keep", bufs=1))
         psum = ctx.enter_context(tc.psum_pool(name="psum", bufs=1))
 
-        def tile(shape, dtype, name):
-            return keep.tile(shape, dtype, name=name, align_bytes=64)
+        def tile(shape, dtype, name, after=None):
+            return keep.tile(shape, dtype, name=name, tag=after or name, align_bytes=64)
 
         offsets = keep.tile([P, J // OFFSETS_PER_COLUMN], U16, name="offsets")
         tab_w = tile([P, T], U32, "tab_w")
         tab_s = tile([P, T], U8, "tab_s")
         wk_raw_w = tile([P, R // 2], I32, "wk_raw_w")
-        wk_raw_s = keep.tile([P, R // 4], I32, name="wk_raw_s", tag="shared", align_bytes=64)
+        wk_raw_s = tile([P, R // 4], I32, "wk_raw_s")
         wk_w = tile([P, 2 * R], U8, "wk_w")
         wk_s = tile([P, R], U8, "wk_s")
-        x_raw = tile([P, PACK, M], F32, "x_raw")
+        x_raw = [tile([P, PACK, GROUP], F32, "x_raw%d" % c) for c in range(M // GROUP)]
         wq_raw = [tile([P, PACK, PASS], F32, "wq_raw%d" % h) for h in range(HALVES)]
 
         nc.vector.memset(tab_s[:, : T // 2].bitcast(I32), 0)
         nc.gpsimd.memset(tab_s[:, T // 2 :].bitcast(I32), 0)
         nc.vector.memset(wk_raw_s[:], 0)
+
+        def load_wq(h):
+            rows = wq[:, h * PASS : (h + 1) * PASS]
+            nc.sync.dma_start(wq_raw[h][:], rows.rearrange("(p code) r -> p code r", code=PACK))
+
+        def load_x(c):
+            cols = x[:, c * GROUP : (c + 1) * GROUP]
+            nc.sync.dma_start(x_raw[c][:], cols.rearrange("(p code) m -> p code m", code=PACK))
 
         nc.sync.dma_start(offsets[:], offs)
         nc.sync.dma_start(wk_raw_w[:], wk_words[0].bitcast(I32))
@@ -92,40 +77,35 @@ def tile_list_kvt_no_scale_kernel(
         nc.sync.dma_start(tab_w[:].bitcast(I32), tab_words[0].rearrange("p t i -> p (t i)").bitcast(I32))
         for row in range(SCALE_ROWS):
             nc.sync.dma_start(wk_raw_s[row:P:QUADRANT, :], wk_scales[0, row:BLOCKS:SCALE_ROWS, :].bitcast(I32))
-        nc.sync.dma_start(x_raw[:], x.rearrange("(p code) m -> p code m", code=PACK))
-        for h in range(HALVES):
-            rows = wq[:, h * PASS : (h + 1) * PASS]
-            nc.sync.dma_start(wq_raw[h][:], rows.rearrange("(p code) r -> p code r", code=PACK))
+        load_x(0)
+        load_x(1)
+        load_wq(0)
+        load_wq(1)
 
-        got_w = [tile([P, SLICE], U32, "got_w0")]
-        got_s = [tile([P, SLICE], U8, "got_s%d" % n) for n in range(J // SLICE)]
-        banks = [psum.tile([P, BANK], F32, name="bank%d" % b) for b in range(8)]
-        banks_taken = {S: 0, V: 0}
+        got_w, got_s = [], []
+        banks = [psum.tile([P, BANK], F32, name="bank%d" % b) for b in range(BANKS)]
+        taken = []
 
         def operand(width, name):
-            return (
-                tile([P, PACK * width], BF16, name + "_bf"),
-                tile([P, width], U32, name + "_w"),
-                tile([P, width], U8, name + "_s"),
-            )
+            return [tile([P, PACK * width], BF16, name + "_bf"), name]
 
-        x_op = operand(M, "x")
+        x_op = [operand(GROUP, "x%d" % c) for c in range(M // GROUP)]
         wq_op = [operand(PASS, "wq%d" % h) for h in range(HALVES)]
-        q_op = [operand(M, "q%d" % h) for h in range(HALVES)]
-        k_op = [[operand(width, "k%d_%d" % (g, h)) for h in range(HALVES)] for g, (j0, width) in enumerate(GROUPS)]
+        q_op = [operand(HALVES * GROUP, "q%d" % c) for c in range(M // GROUP)]
+        k_op = [operand(HALVES * GROUP, "k%d" % g) for g in range(J // GROUP)]
         out_tiles = out.rearrange("(a p) j -> p a j", p=P)
 
         def list_slice(n):
             columns = SLICE // OFFSETS_PER_COLUMN
             return offsets[:, n * columns : (n + 1) * columns]
 
-        def gather_scales(n):
+        def gather_scales(n, after=None):
+            got_s.append(tile([P, SLICE], U8, "got_s%d" % n, after))
             nc.vector.tensor_copy(got_s[n][:], tab_s[:].indirect(list_slice(n)))
 
-        def gather_words(n):
-            if n == WORD_TILES - 1:
-                got_w.append(keep.tile([P, SLICE], U32, name="got_w1", tag="shared", align_bytes=64))
-            nc.vector.tensor_copy(got_w[n % WORD_TILES][:], tab_w[:].indirect(list_slice(n)))
+        def gather_words(n, after=None):
+            got_w.append(tile([P, SLICE], U32, "got_w%d" % n, after))
+            nc.vector.tensor_copy(got_w[n][:], tab_w[:].indirect(list_slice(n)))
 
         def order_columns(ordered, raw, elements_per_run):
             nc.vector.tensor_copy(
@@ -133,34 +113,32 @@ def tile_list_kvt_no_scale_kernel(
                 raw[:].rearrange("p (h c t e) -> p h t c e", h=HALVES, t=PACK, e=elements_per_run),
             )
 
-        def round_x():
-            nc.vector.tensor_copy(
-                x_op[0][:].rearrange("p (c i code) -> p c code i", i=RUN, code=PACK),
-                x_raw[:].rearrange("p code (c i) -> p c code i", i=RUN),
-            )
+        def round_x(c):
+            dst = x_op[c][0][:].rearrange("p (c i code) -> p c code i", i=RUN, code=PACK)
+            src = x_raw[c][:].rearrange("p code (c i) -> p c code i", i=RUN)
+            nc.vector.tensor_copy(dst, src)
 
         def round_wq(h):
-            nc.vector.tensor_copy(
-                wq_op[h][0][:].rearrange("p (t c i code) -> p t c code i", t=PACK, i=RUN, code=PACK),
-                wq_raw[h][:].rearrange("p code (c t i) -> p t c code i", t=PACK, i=RUN),
-            )
+            dst = wq_op[h][0][:].rearrange("p (t c i code) -> p t c code i", t=PACK, i=RUN, code=PACK)
+            src = wq_raw[h][:].rearrange("p code (c t i) -> p t c code i", t=PACK, i=RUN)
+            nc.vector.tensor_copy(dst, src)
 
-        def quantise(op, first, width):
-            values, words, scales = op
-            nc.vector.quantize_mx(
-                out=words[:, first : first + width].bitcast(FP8X4),
-                scales=scales[:, first : first + width],
-                in_=values[:, PACK * first : PACK * (first + width)],
-            )
+        def quantise(op, after=None):
+            values, name = op
+            words = tile([P, values.shape[1] // PACK], U32, name + "_w", after)
+            scales = tile([P, values.shape[1] // PACK], U8, name + "_s")
+            op[1:] = [words, scales]
+            nc.vector.quantize_mx(out=words[:].bitcast(FP8X4), scales=scales[:], in_=values[:])
 
-        def take_bank(engine):
-            own = BANKS_OF[engine]
-            bank = banks[own[banks_taken[engine] % len(own)]]
-            banks_taken[engine] += 1
-            return bank
+        def take_bank():
+            taken.append(banks[len(taken) % BANKS])
+            return taken[-1]
 
-        def project(weights, moving_w, moving_s, values, engine, as_activation):
-            bank = take_bank(engine)
+        def on_vector():
+            return len(taken) > VECTOR_FROM and len(taken) % VECTOR_EVERY == 0 or len(taken) == 56
+
+        def project(weights, moving_w, moving_s, values):
+            bank = take_bank()
             for t in range(PACK):
                 nc.tensor.matmul_mx(
                     out=bank[:, t * BLOCK : (t + 1) * BLOCK], lhsT=weights[t][0], lhsT_scale=weights[t][1],
@@ -168,68 +146,94 @@ def tile_list_kvt_no_scale_kernel(
                 )
             dst = values.rearrange("p (n t) -> p n t", t=PACK)
             src = bank[:].rearrange("p (t n) -> p n t", t=PACK)
-            if engine == V:
+            if on_vector():
                 nc.vector.tensor_copy(dst, src)
-            elif as_activation:
+            elif len(taken) == 1:
                 nc.scalar.activation(dst, src, COPY)
             else:
                 nc.scalar.copy(dst, src)
 
-        def queries(h, block, engine):
+        def queries(c, step):
+            h, block = divmod(step, GROUP // BLOCK)
             weights = [
                 (wq_op[h][1][:, t * P : (t + 1) * P].bitcast(FP8X4), wq_op[h][2][:, t * P : (t + 1) * P])
                 for t in range(PACK)
             ]
             cols = slice(block * BLOCK, (block + 1) * BLOCK)
-            values = q_op[h][0][:, PACK * cols.start : PACK * cols.stop]
-            project(weights, x_op[1][:, cols], x_op[2][:, cols], values, engine, False)
+            values = q_op[c][0][:, step * BANK : (step + 1) * BANK]
+            project(weights, x_op[c][1][:, cols], x_op[c][2][:, cols], values)
 
-        def keys(g, h, block, engine):
+        def keys(g, step):
+            h, block = divmod(step, GROUP // BLOCK)
             firsts = [h * PASS + t * P for t in range(PACK)]
             weights = [(wk_w[:, 2 * r0 : 2 * (r0 + P)].bitcast(FP4X4), wk_s[:, r0 : r0 + P]) for r0 in firsts]
-            n, at = divmod(GROUPS[g][0] + block * BLOCK, SLICE)
+            n, at = divmod(g * GROUP + block * BLOCK, SLICE)
             cols = slice(at, at + BLOCK)
-            values = k_op[g][h][0][:, PACK * block * BLOCK : PACK * (block + 1) * BLOCK]
-            as_activation = (g, h, block) == FIRST_KEYS
-            project(weights, got_w[n % WORD_TILES][:, cols], got_s[n][:, cols], values, engine, as_activation)
+            values = k_op[g][0][:, step * BANK : (step + 1) * BANK]
+            project(weights, got_w[n][:, cols], got_s[n][:, cols], values)
 
-        def scores(g, b, engine):
-            j0, width = GROUPS[g]
-            per_bank = BANK // width
-            bank = take_bank(engine)
-            for slot in range(per_bank):
-                rows = slice((b * per_bank + slot) * P, (b * per_bank + slot + 1) * P)
+        def scores(g, c):
+            bank = take_bank()
+            for slot in range(GROUP // P):
                 for h in range(HALVES):
+                    rows = slice(h * GROUP + slot * P, h * GROUP + (slot + 1) * P)
+                    cols = slice(h * GROUP, (h + 1) * GROUP)
                     nc.tensor.matmul_mx(
-                        out=bank[:, slot * width : (slot + 1) * width],
-                        lhsT=q_op[h][1][:, rows].bitcast(FP8X4), lhsT_scale=q_op[h][2][:, rows],
-                        rhs=k_op[g][h][1][:].bitcast(FP8X4), rhs_scale=k_op[g][h][2][:],
+                        out=bank[:, slot * GROUP : (slot + 1) * GROUP],
+                        lhsT=q_op[c][1][:, rows].bitcast(FP8X4), lhsT_scale=q_op[c][2][:, rows],
+                        rhs=k_op[g][1][:, cols].bitcast(FP8X4), rhs_scale=k_op[g][2][:, cols],
                         start=(h == 0), stop=(h == HALVES - 1),
                     )
-            result = tile([P, BANK], F32, "res%d_%d" % (g, b))
-            if engine == V:
+            result = tile([P, BANK], F32, "res%d_%d" % (g, c))
+            if on_vector():
                 nc.vector.tensor_scalar(result[:], bank[:], SCORE_SCALE, None, MULT)
             else:
                 nc.scalar.activation(result[:], bank[:], COPY, scale=SCORE_SCALE)
+            per_bank = BANK // GROUP
             nc.sync.dma_start(
-                out_tiles[:, b * per_bank : (b + 1) * per_bank, j0 : j0 + width],
+                out_tiles[:, c * per_bank : (c + 1) * per_bank, g * GROUP : (g + 1) * GROUP],
                 result[:].rearrange("p (a j) -> p a j", a=per_bank),
             )
 
-        steps = {
-            "order wk words": lambda: order_columns(wk_w, wk_raw_w, 2),
-            "order wk scales": lambda: order_columns(wk_s, wk_raw_s, 1),
-            "gather scales": gather_scales,
-            "gather words": gather_words,
-            "round x": round_x,
-            "round wq": round_wq,
-            "quantise x": lambda: quantise(x_op, 0, M),
-            "quantise wq": lambda h: quantise(wq_op[h], 0, PASS),
-            "quantise q": lambda h, half: quantise(q_op[h], half * M // 2, M // 2),
-            "quantise k": lambda g, h: quantise(k_op[g][h], 0, GROUPS[g][1]),
-            "queries": queries,
-            "keys": keys,
-            "scores": scores,
-        }
-        for step in ORDER:
-            steps[step[0]](*step[1:])
+        order_columns(wk_w, wk_raw_w, 2)
+        for n in range(J // SLICE):
+            gather_scales(n)
+        gather_words(0)
+        order_columns(wk_s, wk_raw_s, 1)
+        gather_words(1, "wk_raw_s")
+        for c in range(M // GROUP):
+            round_x(c)
+        for h in range(HALVES):
+            round_wq(h)
+        for c in range(M // GROUP):
+            quantise(x_op[c])
+        for h in range(HALVES):
+            quantise(wq_op[h])
+
+        steps = HALVES * GROUP // BLOCK
+        key_steps = J // GROUP * steps
+        score_steps = J // GROUP * (M // GROUP)
+        done = 0
+        for k in range(key_steps):
+            g, step = divmod(k, steps)
+            keys(g, step)
+            if step == 0 and g > 0:
+                quantise(k_op[g - 1], {1: "wq_raw0", 2: "wq_raw1"}.get(g))
+            if k == 11:
+                gather_words(2, "wq1_bf")
+            if k == 17:
+                gather_words(3, "wk_raw_s")
+            if k in QUERIES_AT:
+                h = QUERIES_AT.index(k)
+                for c in range(M // GROUP):
+                    for block in range(GROUP // BLOCK):
+                        queries(c, h * (GROUP // BLOCK) + block)
+            if k == QUERIES_AT[-1] + 1:
+                for c in range(M // GROUP):
+                    quantise(q_op[c])
+            if k >= SCORES_FROM:
+                scores(*divmod(done, M // GROUP))
+                done = done + 1
+        quantise(k_op[-1])
+        for s in range(done, score_steps):
+            scores(*divmod(s, M // GROUP))

@@ -29,10 +29,10 @@ BANKS = 8
 BLOCK = BANK // PACK
 GROUP = 256
 SLICE = 512
+WIDTHS = [256] * 7 + [128] * 2
+FIRSTS = [sum(WIDTHS[:g]) for g in range(len(WIDTHS))]
 OFFSETS_PER_COLUMN = 16
 SCORE_SCALE = 0.03125
-VECTOR_FROM = 14
-VECTOR_EVERY = 4
 QUERIES_AT = (10,11)
 SCORES_FROM = 19
 
@@ -55,7 +55,7 @@ def tile_list_kvt_no_scale_kernel(
         wk_raw_s = tile([P, R // 4], I32, "wk_raw_s")
         wk_w = tile([P, 2 * R], U8, "wk_w")
         wk_s = tile([P, R], U8, "wk_s")
-        x_raw = [tile([P, PACK, GROUP], F32, "x_raw%d" % c) for c in range(M // GROUP)]
+        x_raw = tile([P, PACK, M], F32, "x_raw")
         wq_raw = [tile([P, PACK, PASS], F32, "wq_raw%d" % h) for h in range(HALVES)]
 
         nc.vector.memset(tab_s[:, : T // 2].bitcast(I32), 0)
@@ -66,10 +66,6 @@ def tile_list_kvt_no_scale_kernel(
             rows = wq[:, h * PASS : (h + 1) * PASS]
             nc.sync.dma_start(wq_raw[h][:], rows.rearrange("(p code) r -> p code r", code=PACK))
 
-        def load_x(c):
-            cols = x[:, c * GROUP : (c + 1) * GROUP]
-            nc.sync.dma_start(x_raw[c][:], cols.rearrange("(p code) m -> p code m", code=PACK))
-
         nc.sync.dma_start(offsets[:], offs)
         nc.sync.dma_start(wk_raw_w[:], wk_words[0].bitcast(I32))
         for row in range(SCALE_ROWS):
@@ -77,8 +73,7 @@ def tile_list_kvt_no_scale_kernel(
         nc.sync.dma_start(tab_w[:].bitcast(I32), tab_words[0].rearrange("p t i -> p (t i)").bitcast(I32))
         for row in range(SCALE_ROWS):
             nc.sync.dma_start(wk_raw_s[row:P:QUADRANT, :], wk_scales[0, row:BLOCKS:SCALE_ROWS, :].bitcast(I32))
-        load_x(0)
-        load_x(1)
+        nc.sync.dma_start(x_raw[:], x.rearrange("(p code) m -> p code m", code=PACK))
         load_wq(0)
         load_wq(1)
 
@@ -89,10 +84,10 @@ def tile_list_kvt_no_scale_kernel(
         def operand(width, name):
             return [tile([P, PACK * width], BF16, name + "_bf"), name]
 
-        x_op = [operand(GROUP, "x%d" % c) for c in range(M // GROUP)]
+        x_op = operand(M, "x")
         wq_op = [operand(PASS, "wq%d" % h) for h in range(HALVES)]
         q_op = [operand(HALVES * GROUP, "q%d" % c) for c in range(M // GROUP)]
-        k_op = [operand(HALVES * GROUP, "k%d" % g) for g in range(J // GROUP)]
+        k_op = [operand(HALVES * width, "k%d" % g) for g, width in enumerate(WIDTHS)]
         out_tiles = out.rearrange("(a p) j -> p a j", p=P)
 
         def list_slice(n):
@@ -100,8 +95,10 @@ def tile_list_kvt_no_scale_kernel(
             return offsets[:, n * columns : (n + 1) * columns]
 
         def gather_scales(n, after=None):
-            got_s.append(tile([P, SLICE], U8, "got_s%d" % n, after))
-            nc.vector.tensor_copy(got_s[n][:], tab_s[:].indirect(list_slice(n)))
+            got = tile([P, 2 * SLICE], U8, "got_s%d" % n, after)
+            got_s.extend([got[:, :SLICE], got[:, SLICE:]])
+            columns = SLICE // OFFSETS_PER_COLUMN
+            nc.vector.tensor_copy(got[:], tab_s[:].indirect(offsets[:, n * columns : (n + 2) * columns]))
 
         def gather_words(n, after=None):
             got_w.append(tile([P, SLICE], U32, "got_w%d" % n, after))
@@ -113,9 +110,9 @@ def tile_list_kvt_no_scale_kernel(
                 raw[:].rearrange("p (h c t e) -> p h t c e", h=HALVES, t=PACK, e=elements_per_run),
             )
 
-        def round_x(c):
-            dst = x_op[c][0][:].rearrange("p (c i code) -> p c code i", i=RUN, code=PACK)
-            src = x_raw[c][:].rearrange("p code (c i) -> p c code i", i=RUN)
+        def round_x():
+            dst = x_op[0][:].rearrange("p (c i code) -> p c code i", i=RUN, code=PACK)
+            src = x_raw[:].rearrange("p code (c i) -> p c code i", i=RUN)
             nc.vector.tensor_copy(dst, src)
 
         def round_wq(h):
@@ -135,7 +132,8 @@ def tile_list_kvt_no_scale_kernel(
             return taken[-1]
 
         def on_vector():
-            return len(taken) > VECTOR_FROM and len(taken) % VECTOR_EVERY == 0 or len(taken) == 56
+            n = len(taken)
+            return n > 14 and n % (4 if n <= 50 else 2) == 0
 
         def project(weights, moving_w, moving_s, values):
             bank = take_bank()
@@ -159,63 +157,60 @@ def tile_list_kvt_no_scale_kernel(
                 (wq_op[h][1][:, t * P : (t + 1) * P].bitcast(FP8X4), wq_op[h][2][:, t * P : (t + 1) * P])
                 for t in range(PACK)
             ]
-            cols = slice(block * BLOCK, (block + 1) * BLOCK)
+            cols = slice(c * GROUP + block * BLOCK, c * GROUP + (block + 1) * BLOCK)
             values = q_op[c][0][:, step * BANK : (step + 1) * BANK]
-            project(weights, x_op[c][1][:, cols], x_op[c][2][:, cols], values)
+            project(weights, x_op[1][:, cols], x_op[2][:, cols], values)
 
         def keys(g, step):
-            h, block = divmod(step, GROUP // BLOCK)
+            h, block = divmod(step, WIDTHS[g] // BLOCK)
             firsts = [h * PASS + t * P for t in range(PACK)]
             weights = [(wk_w[:, 2 * r0 : 2 * (r0 + P)].bitcast(FP4X4), wk_s[:, r0 : r0 + P]) for r0 in firsts]
-            n, at = divmod(g * GROUP + block * BLOCK, SLICE)
+            n, at = divmod(FIRSTS[g] + block * BLOCK, SLICE)
             cols = slice(at, at + BLOCK)
             values = k_op[g][0][:, step * BANK : (step + 1) * BANK]
             project(weights, got_w[n][:, cols], got_s[n][:, cols], values)
 
         def scores(g, c):
-            bank = take_bank()
+            width = WIDTHS[g]
+            bank = take_bank()[:, : GROUP // P * width]
             for slot in range(GROUP // P):
                 for h in range(HALVES):
                     rows = slice(h * GROUP + slot * P, h * GROUP + (slot + 1) * P)
-                    cols = slice(h * GROUP, (h + 1) * GROUP)
+                    cols = slice(h * width, (h + 1) * width)
                     nc.tensor.matmul_mx(
-                        out=bank[:, slot * GROUP : (slot + 1) * GROUP],
+                        out=bank[:, slot * width : (slot + 1) * width],
                         lhsT=q_op[c][1][:, rows].bitcast(FP8X4), lhsT_scale=q_op[c][2][:, rows],
                         rhs=k_op[g][1][:, cols].bitcast(FP8X4), rhs_scale=k_op[g][2][:, cols],
                         start=(h == 0), stop=(h == HALVES - 1),
                     )
-            result = tile([P, BANK], F32, "res%d_%d" % (g, c))
+            result = tile([P, GROUP // P * width], F32, "res%d_%d" % (g, c))
             if on_vector():
-                nc.vector.tensor_scalar(result[:], bank[:], SCORE_SCALE, None, MULT)
+                nc.vector.tensor_scalar(result[:], bank, SCORE_SCALE, None, MULT)
             else:
-                nc.scalar.activation(result[:], bank[:], COPY, scale=SCORE_SCALE)
-            per_bank = BANK // GROUP
+                nc.scalar.activation(result[:], bank, COPY, scale=SCORE_SCALE)
+            per_bank = GROUP // P
             nc.sync.dma_start(
-                out_tiles[:, c * per_bank : (c + 1) * per_bank, g * GROUP : (g + 1) * GROUP],
+                out_tiles[:, c * per_bank : (c + 1) * per_bank, FIRSTS[g] : FIRSTS[g] + width],
                 result[:].rearrange("p (a j) -> p a j", a=per_bank),
             )
 
         order_columns(wk_w, wk_raw_w, 2)
-        for n in range(J // SLICE):
+        for n in range(0, J // SLICE, 2):
             gather_scales(n)
         gather_words(0)
         order_columns(wk_s, wk_raw_s, 1)
         gather_words(1, "wk_raw_s")
-        for c in range(M // GROUP):
-            round_x(c)
+        round_x()
         for h in range(HALVES):
             round_wq(h)
-        for c in range(M // GROUP):
-            quantise(x_op[c])
+        quantise(x_op)
         for h in range(HALVES):
             quantise(wq_op[h])
 
-        steps = HALVES * GROUP // BLOCK
-        key_steps = J // GROUP * steps
-        score_steps = J // GROUP * (M // GROUP)
+        key_steps = [(g, step) for g, width in enumerate(WIDTHS) for step in range(HALVES * width // BLOCK)]
+        score_steps = [(g, c) for g in range(len(WIDTHS)) for c in range(M // GROUP)]
         done = 0
-        for k in range(key_steps):
-            g, step = divmod(k, steps)
+        for k, (g, step) in enumerate(key_steps):
             keys(g, step)
             if step == 0 and g > 0:
                 quantise(k_op[g - 1], {1: "wq_raw0", 2: "wq_raw1"}.get(g))
@@ -232,8 +227,8 @@ def tile_list_kvt_no_scale_kernel(
                 for c in range(M // GROUP):
                     quantise(q_op[c])
             if k >= SCORES_FROM:
-                scores(*divmod(done, M // GROUP))
+                scores(*score_steps[done])
                 done = done + 1
         quantise(k_op[-1])
-        for s in range(done, score_steps):
-            scores(*divmod(s, M // GROUP))
+        for g, c in score_steps[done:]:
+            scores(g, c)

@@ -34,7 +34,7 @@ FIRSTS = [sum(WIDTHS[:g]) for g in range(len(WIDTHS))]
 OFFSETS_PER_COLUMN = 16
 SCORE_SCALE = 0.03125
 QUERIES_AT = (10,11)
-SCORES_FROM = 19
+SCORES_FROM = 18
 
 
 def tile_list_kvt_no_scale_kernel(
@@ -133,7 +133,7 @@ def tile_list_kvt_no_scale_kernel(
 
         def on_vector():
             n = len(taken)
-            return n > 14 and n % (4 if n <= 50 else 2) == 0
+            return n > 21 and n % (3 if n <= 50 else 2) == 0
 
         def project(weights, moving_w, moving_s, values):
             bank = take_bank()
@@ -213,9 +213,9 @@ def tile_list_kvt_no_scale_kernel(
         for k, (g, step) in enumerate(key_steps):
             keys(g, step)
             if step == 0 and g > 0:
-                quantise(k_op[g - 1], {1: "wq_raw0", 2: "wq_raw1"}.get(g))
+                quantise(k_op[g - 1], {1: "wq_raw1", 2: "wq1_bf"}.get(g))
             if k == 11:
-                gather_words(2, "wq1_bf")
+                gather_words(2, "k0_bf")
             if k == 17:
                 gather_words(3, "wk_raw_s")
             if k in QUERIES_AT:

@@ -24,6 +24,7 @@ RUN = 4
 QUADRANT = 32
 SCALE_ROWS = 4
 BLOCKS = PASS // 32
+PARKED = P - BLOCKS
 BANK = 512
 BANKS = 8
 BLOCK = BANK // PACK
@@ -58,26 +59,44 @@ def tile_list_kvt_no_scale_kernel(
         x_raw = tile([P, PACK, M], F32, "x_raw")
         wq_raw = [tile([P, PACK, PASS], F32, "wq_raw%d" % h) for h in range(HALVES)]
 
-        nc.vector.memset(tab_s[:, : T // 2].bitcast(I32), 0)
-        nc.gpsimd.memset(tab_s[:, T // 2 :].bitcast(I32), 0)
-        nc.vector.memset(wk_raw_s[:], 0)
+        plane = [tile([P, J // 2], U8, "plane%d" % n) for n in range(2)]
+        nc.vector.memset(tab_s[:PARKED, :].bitcast(I32), 0)
+        nc.gpsimd.memset(wk_raw_s[:], 0)
+        for n in range(2):
+            nc.gpsimd.memset(plane[n][:].bitcast(I32), 0)
 
         def load_wq(h):
             rows = wq[:, h * PASS : (h + 1) * PASS]
             nc.sync.dma_start(wq_raw[h][:], rows.rearrange("(p code) r -> p code r", code=PACK))
 
+        parked = []
+
+        def gather_scales(n):
+            parked.append(tile([P, J // 2], U8, "parked%d" % n))
+            columns = J // 2 // OFFSETS_PER_COLUMN
+            nc.vector.tensor_copy(parked[n][:], tab_s[:].indirect(offsets[:, n * columns : (n + 1) * columns]))
+
+        def move_scales(n):
+            for q in range(P // QUADRANT):
+                nc.sync.dma_start(
+                    plane[n][q * QUADRANT : q * QUADRANT + SCALE_ROWS, :].bitcast(I32),
+                    parked[n][PARKED + q * SCALE_ROWS : PARKED + (q + 1) * SCALE_ROWS, :].bitcast(I32),
+                )
+
         nc.sync.dma_start(offsets[:], offs)
+        nc.sync.dma_start(tab_s[PARKED:, :].bitcast(I32), tab_scales[0].bitcast(I32))
         nc.sync.dma_start(wk_raw_w[:], wk_words[0].bitcast(I32))
         for row in range(SCALE_ROWS):
-            nc.sync.dma_start(tab_s[row:P:QUADRANT, :].bitcast(I32), tab_scales[0, row:BLOCKS:SCALE_ROWS, :].bitcast(I32))
-        nc.sync.dma_start(tab_w[:].bitcast(I32), tab_words[0].rearrange("p t i -> p (t i)").bitcast(I32))
-        for row in range(SCALE_ROWS):
             nc.sync.dma_start(wk_raw_s[row:P:QUADRANT, :], wk_scales[0, row:BLOCKS:SCALE_ROWS, :].bitcast(I32))
+        nc.sync.dma_start(tab_w[:].bitcast(I32), tab_words[0].rearrange("p t i -> p (t i)").bitcast(I32))
+        gather_scales(0)
+        move_scales(0)
         nc.sync.dma_start(x_raw[:], x.rearrange("(p code) m -> p code m", code=PACK))
         load_wq(0)
         load_wq(1)
 
-        got_w, got_s = [], []
+        got_w = []
+        got_s = [plane[n // 2][:, n % 2 * SLICE : (n % 2 + 1) * SLICE] for n in range(J // SLICE)]
         banks = [psum.tile([P, BANK], F32, name="bank%d" % b) for b in range(BANKS)]
         taken = []
 
@@ -94,18 +113,12 @@ def tile_list_kvt_no_scale_kernel(
             columns = SLICE // OFFSETS_PER_COLUMN
             return offsets[:, n * columns : (n + 1) * columns]
 
-        def gather_scales(n, after=None):
-            got = tile([P, 2 * SLICE], U8, "got_s%d" % n, after)
-            got_s.extend([got[:, :SLICE], got[:, SLICE:]])
-            columns = SLICE // OFFSETS_PER_COLUMN
-            nc.vector.tensor_copy(got[:], tab_s[:].indirect(offsets[:, n * columns : (n + 2) * columns]))
-
         def gather_words(n, after=None):
             got_w.append(tile([P, SLICE], U32, "got_w%d" % n, after))
             nc.vector.tensor_copy(got_w[n][:], tab_w[:].indirect(list_slice(n)))
 
-        def order_columns(ordered, raw, elements_per_run):
-            nc.vector.tensor_copy(
+        def order_columns(engine, ordered, raw, elements_per_run):
+            engine.tensor_copy(
                 ordered[:].bitcast(I32).rearrange("p (h t c e) -> p h t c e", h=HALVES, t=PACK, e=elements_per_run),
                 raw[:].rearrange("p (h c t e) -> p h t c e", h=HALVES, t=PACK, e=elements_per_run),
             )
@@ -170,21 +183,28 @@ def tile_list_kvt_no_scale_kernel(
             values = k_op[g][0][:, step * BANK : (step + 1) * BANK]
             project(weights, got_w[n][:, cols], got_s[n][:, cols], values)
 
-        def scores(g, c):
+        def score_pass(bank, g, c, slot, h, start, stop):
             width = WIDTHS[g]
-            bank = take_bank()[:, : GROUP // P * width]
+            rows = slice(h * GROUP + slot * P, h * GROUP + (slot + 1) * P)
+            cols = slice(h * width, (h + 1) * width)
+            nc.tensor.matmul_mx(
+                out=bank[:, slot * width : (slot + 1) * width],
+                lhsT=q_op[c][1][:, rows].bitcast(FP8X4), lhsT_scale=q_op[c][2][:, rows],
+                rhs=k_op[g][1][:, cols].bitcast(FP8X4), rhs_scale=k_op[g][2][:, cols],
+                start=start, stop=stop,
+            )
+
+        def scores(g, c):
+            bank = take_bank()[:, : GROUP // P * WIDTHS[g]]
             for slot in range(GROUP // P):
                 for h in range(HALVES):
-                    rows = slice(h * GROUP + slot * P, h * GROUP + (slot + 1) * P)
-                    cols = slice(h * width, (h + 1) * width)
-                    nc.tensor.matmul_mx(
-                        out=bank[:, slot * width : (slot + 1) * width],
-                        lhsT=q_op[c][1][:, rows].bitcast(FP8X4), lhsT_scale=q_op[c][2][:, rows],
-                        rhs=k_op[g][1][:, cols].bitcast(FP8X4), rhs_scale=k_op[g][2][:, cols],
-                        start=(h == 0), stop=(h == HALVES - 1),
-                    )
+                    score_pass(bank, g, c, slot, h, h == 0, h == HALVES - 1)
+            store(bank, g, c, on_vector())
+
+        def store(bank, g, c, vector):
+            width = WIDTHS[g]
             result = tile([P, GROUP // P * width], F32, "res%d_%d" % (g, c))
-            if on_vector():
+            if vector:
                 nc.vector.tensor_scalar(result[:], bank, SCORE_SCALE, None, MULT)
             else:
                 nc.scalar.activation(result[:], bank, COPY, scale=SCORE_SCALE)
@@ -194,12 +214,12 @@ def tile_list_kvt_no_scale_kernel(
                 result[:].rearrange("p (a j) -> p a j", a=per_bank),
             )
 
-        order_columns(wk_w, wk_raw_w, 2)
-        for n in range(0, J // SLICE, 2):
-            gather_scales(n)
+        order_columns(nc.vector, wk_w, wk_raw_w, 2)
+        order_columns(nc.vector, wk_s, wk_raw_s, 1)
+        gather_scales(1)
+        move_scales(1)
         gather_words(0)
-        order_columns(wk_s, wk_raw_s, 1)
-        gather_words(1, "wk_raw_s")
+        gather_words(1)
         round_x()
         for h in range(HALVES):
             round_wq(h)
@@ -217,7 +237,7 @@ def tile_list_kvt_no_scale_kernel(
             if k == 11:
                 gather_words(2, "k0_bf")
             if k == 17:
-                gather_words(3, "wk_raw_s")
+                gather_words(3, "got_w1")
             if k in QUERIES_AT:
                 h = QUERIES_AT.index(k)
                 for c in range(M // GROUP):
@@ -229,6 +249,21 @@ def tile_list_kvt_no_scale_kernel(
             if k >= SCORES_FROM:
                 scores(*score_steps[done])
                 done = done + 1
-        quantise(k_op[-1])
-        for g, c in score_steps[done:]:
+        last = len(WIDTHS) - 1
+        values = k_op[last][0]
+        k_op[last][1:] = [tile([P, HALVES * BLOCK], U32, "last_w"), tile([P, HALVES * BLOCK], U8, "last_s")]
+        for h in range(HALVES):
+            cols = slice(h * BLOCK, (h + 1) * BLOCK)
+            nc.vector.quantize_mx(
+                out=k_op[last][1][:, cols].bitcast(FP8X4), scales=k_op[last][2][:, cols],
+                in_=values[:, h * BANK : (h + 1) * BANK],
+            )
+        for g, c in score_steps[done:-2]:
             scores(g, c)
+        last_banks = [take_bank()[:, : GROUP // P * BLOCK] for c in range(M // GROUP)]
+        for h in range(HALVES):
+            for c in range(M // GROUP):
+                for slot in range(GROUP // P):
+                    score_pass(last_banks[c], last, c, slot, h, h == 0 and slot == 0, h == 1 and slot == 1)
+        for c in range(M // GROUP):
+            store(last_banks[c], last, c, c == 1)

@@ -15,6 +15,7 @@ FP8X4 = mybir.dt.float8_e4m3fn_x4
 FP4X4 = mybir.dt.float4_e2m1fn_x4
 COPY = mybir.ActivationFunctionType.Copy
 MULT = mybir.AluOpType.mult
+ADD = mybir.AluOpType.add
 
 P = 128
 PACK = 4
@@ -34,7 +35,7 @@ WIDTHS = [256] * 7 + [128] * 2
 FIRSTS = [sum(WIDTHS[:g]) for g in range(len(WIDTHS))]
 OFFSETS_PER_COLUMN = 16
 SCORE_SCALE = 0.03125
-QUERIES_AT = (10,11)
+QUERIES_AT = (13, 14)
 SCORES_FROM = 18
 
 
@@ -71,10 +72,15 @@ def tile_list_kvt_no_scale_kernel(
 
         parked = []
 
-        def gather_scales(n):
+        def gather_scales(n, pieces):
             parked.append(tile([P, J // 2], U8, "parked%d" % n))
-            columns = J // 2 // OFFSETS_PER_COLUMN
-            nc.vector.tensor_copy(parked[n][:], tab_s[:].indirect(offsets[:, n * columns : (n + 1) * columns]))
+            width = J // 2 // pieces
+            columns = width // OFFSETS_PER_COLUMN
+            for i in range(pieces):
+                first = (n * pieces + i) * columns
+                nc.vector.tensor_copy(
+                    parked[n][:, i * width : (i + 1) * width], tab_s[:].indirect(offsets[:, first : first + columns])
+                )
 
         def move_scales(n):
             for q in range(P // QUADRANT):
@@ -89,7 +95,7 @@ def tile_list_kvt_no_scale_kernel(
         for row in range(SCALE_ROWS):
             nc.sync.dma_start(wk_raw_s[row:P:QUADRANT, :], wk_scales[0, row:BLOCKS:SCALE_ROWS, :].bitcast(I32))
         nc.sync.dma_start(tab_w[:].bitcast(I32), tab_words[0].rearrange("p t i -> p (t i)").bitcast(I32))
-        gather_scales(0)
+        gather_scales(0, 1)
         move_scales(0)
         nc.sync.dma_start(x_raw[:], x.rearrange("(p code) m -> p code m", code=PACK))
         load_wq(0)
@@ -124,9 +130,8 @@ def tile_list_kvt_no_scale_kernel(
             )
 
         def round_x():
-            dst = x_op[0][:].rearrange("p (c i code) -> p c code i", i=RUN, code=PACK)
-            src = x_raw[:].rearrange("p code (c i) -> p c code i", i=RUN)
-            nc.vector.tensor_copy(dst, src)
+            dst = x_op[0][:].rearrange("p (m code) -> p m code", code=PACK)
+            nc.gpsimd.tensor_scalar(dst, x_raw[:].rearrange("p code m -> p m code"), 1.0, 0.0, MULT, ADD)
 
         def round_wq(h):
             dst = wq_op[h][0][:].rearrange("p (t c i code) -> p t c code i", t=PACK, i=RUN, code=PACK)
@@ -146,7 +151,7 @@ def tile_list_kvt_no_scale_kernel(
 
         def on_vector():
             n = len(taken)
-            return n > 21 and n % (3 if n <= 50 else 2) == 0
+            return n in (2, 4, 6, 8, 23) or n > 31 and n % 5 in (2, 4)
 
         def project(weights, moving_w, moving_s, values):
             bank = take_bank()
@@ -214,39 +219,53 @@ def tile_list_kvt_no_scale_kernel(
                 result[:].rearrange("p (a j) -> p a j", a=per_bank),
             )
 
-        order_columns(nc.vector, wk_w, wk_raw_w, 2)
-        order_columns(nc.vector, wk_s, wk_raw_s, 1)
-        gather_scales(1)
+        order_columns(nc.gpsimd, wk_w, wk_raw_w, 2)
+        order_columns(nc.gpsimd, wk_s, wk_raw_s, 1)
+        gather_scales(1, 2)
+        warm = operand(P, "warm")
+        nc.vector.memset(warm[0][:].bitcast(I32), 0)
+        quantise(warm)
+        for n in range(6):
+            nc.tensor.matmul_mx(
+                out=banks[-1][:], lhsT=warm[1][:].bitcast(FP8X4), lhsT_scale=parked[1][:, :P],
+                rhs=wk_w[:, : 2 * BANK].bitcast(FP4X4), rhs_scale=wk_s[:, :BANK], start=True, stop=True,
+            )
         move_scales(1)
         gather_words(0)
         gather_words(1)
         round_x()
-        for h in range(HALVES):
-            round_wq(h)
-        quantise(x_op)
-        for h in range(HALVES):
-            quantise(wq_op[h])
 
         key_steps = [(g, step) for g, width in enumerate(WIDTHS) for step in range(HALVES * width // BLOCK)]
         score_steps = [(g, c) for g in range(len(WIDTHS)) for c in range(M // GROUP)]
+        score_steps[1:3] = [score_steps[2], score_steps[1]]
         done = 0
         for k, (g, step) in enumerate(key_steps):
             keys(g, step)
-            if step == 0 and g > 0:
-                quantise(k_op[g - 1], {1: "wq_raw1", 2: "wq1_bf"}.get(g))
-            if k == 11:
-                gather_words(2, "k0_bf")
-            if k == 17:
-                gather_words(3, "got_w1")
+            if k == 7:
+                round_wq(0)
+                quantise(x_op, "wq_raw0")
+                quantise(wq_op[0])
+                round_wq(1)
+                quantise(k_op[0], "wq_raw1")
+                quantise(wq_op[1])
+                gather_words(2, "wq1_bf")
             if k in QUERIES_AT:
                 h = QUERIES_AT.index(k)
                 for c in range(M // GROUP):
                     for block in range(GROUP // BLOCK):
                         queries(c, h * (GROUP // BLOCK) + block)
-            if k == QUERIES_AT[-1] + 1:
-                for c in range(M // GROUP):
-                    quantise(q_op[c])
-            if k >= SCORES_FROM:
+                    if h == 1 and c == 0:
+                        quantise(q_op[0])
+            if k == QUERIES_AT[-1]:
+                quantise(k_op[1], "q0_bf")
+                quantise(q_op[1])
+                quantise(k_op[2], "q1_bf")
+            if k == 16:
+                quantise(k_op[3], "k2_bf")
+                gather_words(3, "k3_bf")
+            if step == 0 and g > 4:
+                quantise(k_op[g - 1])
+            for n in range({16: 1, 17: 1, 18: 2, 19: 2, 20: 2, 23: 1, 24: 1, 27: 1, 28: 1, 30: 1, 31: 1}.get(k, 0)):
                 scores(*score_steps[done])
                 done = done + 1
         last = len(WIDTHS) - 1

@@ -48,7 +48,7 @@ def tile_list_kvt_no_scale_kernel(
         psum = ctx.enter_context(tc.psum_pool(name="psum", bufs=1))
 
         def tile(shape, dtype, name, after=None):
-            return keep.tile(shape, dtype, name=name, tag=after or name, align_bytes=64)
+            return keep.tile(shape, dtype, name=name, tag=after or name, align_bytes=256)
 
         offsets = keep.tile([P, J // OFFSETS_PER_COLUMN], U16, name="offsets")
         tab_w = tile([P, T], U32, "tab_w")

@@ -28,15 +28,24 @@ BLOCKS = PASS // 32
 PARKED = P - BLOCKS
 BANK = 512
 BANKS = 8
-BLOCK = BANK // PACK
+STEP = BANK // PACK
 GROUP = 256
 SLICE = 512
-WIDTHS = [256] * 7 + [128] * 2
-FIRSTS = [sum(WIDTHS[:g]) for g in range(len(WIDTHS))]
 OFFSETS_PER_COLUMN = 16
 SCORE_SCALE = 0.03125
+ALIGN = 256
+
+WIDTHS = [GROUP] * 7 + [STEP] * 2
+FIRSTS = [sum(WIDTHS[:g]) for g in range(len(WIDTHS))]
+STEPS_PER_GROUP = HALVES * GROUP // STEP
+
+WARM_UP_PASSES = 7
 QUERIES_AT = (13, 14)
-SCORES_FROM = 18
+EARLY_GROUPS = 4
+SCORES_FROM = 16
+SCORE_LAG = 4
+SHARE_FROM = 31
+SHARE_OF, SHARE = 5, (2, 4)
 
 
 def tile_list_kvt_no_scale_kernel(
@@ -48,7 +57,7 @@ def tile_list_kvt_no_scale_kernel(
         psum = ctx.enter_context(tc.psum_pool(name="psum", bufs=1))
 
         def tile(shape, dtype, name, after=None):
-            return keep.tile(shape, dtype, name=name, tag=after or name, align_bytes=256)
+            return keep.tile(shape, dtype, name=name, tag=after or name, align_bytes=ALIGN)
 
         offsets = keep.tile([P, J // OFFSETS_PER_COLUMN], U16, name="offsets")
         tab_w = tile([P, T], U32, "tab_w")
@@ -59,16 +68,12 @@ def tile_list_kvt_no_scale_kernel(
         wk_s = tile([P, R], U8, "wk_s")
         x_raw = tile([P, PACK, M], F32, "x_raw")
         wq_raw = [tile([P, PACK, PASS], F32, "wq_raw%d" % h) for h in range(HALVES)]
+        key_scales = [tile([P, J // 2], U8, "plane%d" % n) for n in range(2)]
 
-        plane = [tile([P, J // 2], U8, "plane%d" % n) for n in range(2)]
         nc.vector.memset(tab_s[:PARKED, :].bitcast(I32), 0)
         nc.gpsimd.memset(wk_raw_s[:], 0)
         for n in range(2):
-            nc.gpsimd.memset(plane[n][:].bitcast(I32), 0)
-
-        def load_wq(h):
-            rows = wq[:, h * PASS : (h + 1) * PASS]
-            nc.sync.dma_start(wq_raw[h][:], rows.rearrange("(p code) r -> p code r", code=PACK))
+            nc.gpsimd.memset(key_scales[n][:].bitcast(I32), 0)
 
         parked = []
 
@@ -85,7 +90,7 @@ def tile_list_kvt_no_scale_kernel(
         def move_scales(n):
             for q in range(P // QUADRANT):
                 nc.sync.dma_start(
-                    plane[n][q * QUADRANT : q * QUADRANT + SCALE_ROWS, :].bitcast(I32),
+                    key_scales[n][q * QUADRANT : q * QUADRANT + SCALE_ROWS, :].bitcast(I32),
                     parked[n][PARKED + q * SCALE_ROWS : PARKED + (q + 1) * SCALE_ROWS, :].bitcast(I32),
                 )
 
@@ -98,11 +103,12 @@ def tile_list_kvt_no_scale_kernel(
         gather_scales(0, 1)
         move_scales(0)
         nc.sync.dma_start(x_raw[:], x.rearrange("(p code) m -> p code m", code=PACK))
-        load_wq(0)
-        load_wq(1)
+        for h in range(HALVES):
+            columns_of_half = wq[:, h * PASS : (h + 1) * PASS]
+            nc.sync.dma_start(wq_raw[h][:], columns_of_half.rearrange("(p code) r -> p code r", code=PACK))
 
         got_w = []
-        got_s = [plane[n // 2][:, n % 2 * SLICE : (n % 2 + 1) * SLICE] for n in range(J // SLICE)]
+        got_s = [key_scales[n // 2][:, n % 2 * SLICE : (n % 2 + 1) * SLICE] for n in range(J // SLICE)]
         banks = [psum.tile([P, BANK], F32, name="bank%d" % b) for b in range(BANKS)]
         taken = []
 
@@ -115,18 +121,15 @@ def tile_list_kvt_no_scale_kernel(
         k_op = [operand(HALVES * width, "k%d" % g) for g, width in enumerate(WIDTHS)]
         out_tiles = out.rearrange("(a p) j -> p a j", p=P)
 
-        def list_slice(n):
-            columns = SLICE // OFFSETS_PER_COLUMN
-            return offsets[:, n * columns : (n + 1) * columns]
-
         def gather_words(n, after=None):
+            columns = SLICE // OFFSETS_PER_COLUMN
             got_w.append(tile([P, SLICE], U32, "got_w%d" % n, after))
-            nc.vector.tensor_copy(got_w[n][:], tab_w[:].indirect(list_slice(n)))
+            nc.vector.tensor_copy(got_w[n][:], tab_w[:].indirect(offsets[:, n * columns : (n + 1) * columns]))
 
-        def order_columns(engine, ordered, raw, elements_per_run):
-            engine.tensor_copy(
-                ordered[:].bitcast(I32).rearrange("p (h t c e) -> p h t c e", h=HALVES, t=PACK, e=elements_per_run),
-                raw[:].rearrange("p (h c t e) -> p h t c e", h=HALVES, t=PACK, e=elements_per_run),
+        def order_columns(ordered, raw, words_per_run):
+            nc.vector.tensor_copy(
+                ordered[:].bitcast(I32).rearrange("p (h t c e) -> p h t c e", h=HALVES, t=PACK, e=words_per_run),
+                raw[:].rearrange("p (h c t e) -> p h t c e", h=HALVES, t=PACK, e=words_per_run),
             )
 
         def round_x():
@@ -149,99 +152,103 @@ def tile_list_kvt_no_scale_kernel(
             taken.append(banks[len(taken) % BANKS])
             return taken[-1]
 
-        def on_vector():
-            n = len(taken)
-            return n in (2, 4, 6, 8, 23) or n > 31 and n % 5 in (2, 4)
+        def shared_out():
+            return len(taken) > SHARE_FROM and len(taken) % SHARE_OF in SHARE
 
-        def project(weights, moving_w, moving_s, values):
+        def project(weights, moving_w, moving_s, values, on_vector):
             bank = take_bank()
             for t in range(PACK):
                 nc.tensor.matmul_mx(
-                    out=bank[:, t * BLOCK : (t + 1) * BLOCK], lhsT=weights[t][0], lhsT_scale=weights[t][1],
+                    out=bank[:, t * STEP : (t + 1) * STEP], lhsT=weights[t][0], lhsT_scale=weights[t][1],
                     rhs=moving_w.bitcast(FP8X4), rhs_scale=moving_s, start=True, stop=True,
                 )
             dst = values.rearrange("p (n t) -> p n t", t=PACK)
             src = bank[:].rearrange("p (t n) -> p n t", t=PACK)
-            if on_vector():
+            if on_vector or shared_out():
                 nc.vector.tensor_copy(dst, src)
             elif len(taken) == 1:
                 nc.scalar.activation(dst, src, COPY)
             else:
                 nc.scalar.copy(dst, src)
 
-        def queries(c, step):
-            h, block = divmod(step, GROUP // BLOCK)
+        def queries(c, h, part, on_vector):
             weights = [
                 (wq_op[h][1][:, t * P : (t + 1) * P].bitcast(FP8X4), wq_op[h][2][:, t * P : (t + 1) * P])
                 for t in range(PACK)
             ]
-            cols = slice(c * GROUP + block * BLOCK, c * GROUP + (block + 1) * BLOCK)
-            values = q_op[c][0][:, step * BANK : (step + 1) * BANK]
-            project(weights, x_op[1][:, cols], x_op[2][:, cols], values)
+            cols = slice(c * GROUP + part * STEP, c * GROUP + (part + 1) * STEP)
+            step = h * (GROUP // STEP) + part
+            project(weights, x_op[1][:, cols], x_op[2][:, cols], q_op[c][0][:, step * BANK : (step + 1) * BANK], on_vector)
 
-        def keys(g, step):
-            h, block = divmod(step, WIDTHS[g] // BLOCK)
-            firsts = [h * PASS + t * P for t in range(PACK)]
-            weights = [(wk_w[:, 2 * r0 : 2 * (r0 + P)].bitcast(FP4X4), wk_s[:, r0 : r0 + P]) for r0 in firsts]
-            n, at = divmod(FIRSTS[g] + block * BLOCK, SLICE)
-            cols = slice(at, at + BLOCK)
-            values = k_op[g][0][:, step * BANK : (step + 1) * BANK]
-            project(weights, got_w[n][:, cols], got_s[n][:, cols], values)
+        def keys(g, step, on_vector):
+            h, part = divmod(step, WIDTHS[g] // STEP)
+            starts = [h * PASS + t * P for t in range(PACK)]
+            weights = [(wk_w[:, 2 * r0 : 2 * (r0 + P)].bitcast(FP4X4), wk_s[:, r0 : r0 + P]) for r0 in starts]
+            n, at = divmod(FIRSTS[g] + part * STEP, SLICE)
+            cols = slice(at, at + STEP)
+            project(weights, got_w[n][:, cols], got_s[n][:, cols], k_op[g][0][:, step * BANK : (step + 1) * BANK], on_vector)
 
-        def score_pass(bank, g, c, slot, h, start, stop):
+        def score_pass(bank, g, c, a, h, start, stop):
             width = WIDTHS[g]
-            rows = slice(h * GROUP + slot * P, h * GROUP + (slot + 1) * P)
+            rows = slice(h * GROUP + a * P, h * GROUP + (a + 1) * P)
             cols = slice(h * width, (h + 1) * width)
             nc.tensor.matmul_mx(
-                out=bank[:, slot * width : (slot + 1) * width],
+                out=bank[:, a * width : (a + 1) * width],
                 lhsT=q_op[c][1][:, rows].bitcast(FP8X4), lhsT_scale=q_op[c][2][:, rows],
                 rhs=k_op[g][1][:, cols].bitcast(FP8X4), rhs_scale=k_op[g][2][:, cols],
                 start=start, stop=stop,
             )
 
-        def scores(g, c):
-            bank = take_bank()[:, : GROUP // P * WIDTHS[g]]
-            for slot in range(GROUP // P):
-                for h in range(HALVES):
-                    score_pass(bank, g, c, slot, h, h == 0, h == HALVES - 1)
-            store(bank, g, c, on_vector())
-
-        def store(bank, g, c, vector):
+        def store(bank, g, c, on_vector):
             width = WIDTHS[g]
-            result = tile([P, GROUP // P * width], F32, "res%d_%d" % (g, c))
-            if vector:
+            row_tiles = GROUP // P
+            result = tile([P, row_tiles * width], F32, "res%d_%d" % (g, c))
+            if on_vector:
                 nc.vector.tensor_scalar(result[:], bank, SCORE_SCALE, None, MULT)
             else:
                 nc.scalar.activation(result[:], bank, COPY, scale=SCORE_SCALE)
-            per_bank = GROUP // P
             nc.sync.dma_start(
-                out_tiles[:, c * per_bank : (c + 1) * per_bank, FIRSTS[g] : FIRSTS[g] + width],
-                result[:].rearrange("p (a j) -> p a j", a=per_bank),
+                out_tiles[:, c * row_tiles : (c + 1) * row_tiles, FIRSTS[g] : FIRSTS[g] + width],
+                result[:].rearrange("p (a j) -> p a j", a=row_tiles),
             )
 
-        order_columns(nc.gpsimd, wk_w, wk_raw_w, 2)
-        order_columns(nc.gpsimd, wk_s, wk_raw_s, 1)
+        def scores(g, c):
+            bank = take_bank()[:, : GROUP // P * WIDTHS[g]]
+            for a in range(GROUP // P):
+                for h in range(HALVES):
+                    score_pass(bank, g, c, a, h, h == 0, h == HALVES - 1)
+            store(bank, g, c, shared_out())
+
+        order_columns(wk_w, wk_raw_w, 2)
+        order_columns(wk_s, wk_raw_s, 1)
         gather_scales(1, 2)
+
         warm = operand(P, "warm")
         nc.vector.memset(warm[0][:].bitcast(I32), 0)
         quantise(warm)
-        for n in range(6):
+        for n in range(WARM_UP_PASSES):
             nc.tensor.matmul_mx(
-                out=banks[-1][:], lhsT=warm[1][:].bitcast(FP8X4), lhsT_scale=parked[1][:, :P],
-                rhs=wk_w[:, : 2 * BANK].bitcast(FP4X4), rhs_scale=wk_s[:, :BANK], start=True, stop=True,
+                out=banks[-1][:], lhsT=warm[1][:].bitcast(FP8X4), lhsT_scale=warm[2][:],
+                rhs=wk_raw_w[:, : BANK // 2].bitcast(FP4X4), rhs_scale=parked[1][:, :BANK], start=True, stop=True,
             )
         move_scales(1)
         gather_words(0)
         gather_words(1)
         round_x()
 
-        key_steps = [(g, step) for g, width in enumerate(WIDTHS) for step in range(HALVES * width // BLOCK)]
-        score_steps = [(g, c) for g in range(len(WIDTHS)) for c in range(M // GROUP)]
-        score_steps[1:3] = [score_steps[2], score_steps[1]]
-        done = 0
+        key_steps = [(g, step) for g, width in enumerate(WIDTHS) for step in range(HALVES * width // STEP)]
+        last_key_step = len(key_steps) - 1
+        early = [(g, c) for g in range(EARLY_GROUPS) for c in range(M // GROUP)]
+        early[1:3] = [early[2], early[1]]
+        placed = [(SCORES_FROM + min(n, n // 2 + 1), g, c) for n, (g, c) in enumerate(early)]
+        for g in range(EARLY_GROUPS, WIDTHS.index(STEP)):
+            for c in range(M // GROUP):
+                behind = (g + 1) * STEPS_PER_GROUP - 1 + SCORE_LAG + c
+                placed.append((min(behind, last_key_step), g, c))
+
         for k, (g, step) in enumerate(key_steps):
-            keys(g, step)
-            if k == 7:
+            keys(g, step, k < BANKS and k % 2 == 1)
+            if k == BANKS - 1:
                 round_wq(0)
                 quantise(x_op, "wq_raw0")
                 quantise(wq_op[0])
@@ -252,37 +259,38 @@ def tile_list_kvt_no_scale_kernel(
             if k in QUERIES_AT:
                 h = QUERIES_AT.index(k)
                 for c in range(M // GROUP):
-                    for block in range(GROUP // BLOCK):
-                        queries(c, h * (GROUP // BLOCK) + block)
-                    if h == 1 and c == 0:
+                    for part in range(GROUP // STEP):
+                        queries(c, h, part, (h, c, part) == (1, 1, 1))
+                    if (h, c) == (1, 0):
                         quantise(q_op[0])
             if k == QUERIES_AT[-1]:
                 quantise(k_op[1], "q0_bf")
                 quantise(q_op[1])
                 quantise(k_op[2], "q1_bf")
-            if k == 16:
-                quantise(k_op[3], "k2_bf")
+            if k == EARLY_GROUPS * STEPS_PER_GROUP:
+                quantise(k_op[EARLY_GROUPS - 1], "k2_bf")
                 gather_words(3, "k3_bf")
-            if step == 0 and g > 4:
+            if step == 0 and g > EARLY_GROUPS:
                 quantise(k_op[g - 1])
-            for n in range({16: 1, 17: 1, 18: 2, 19: 2, 20: 2, 23: 1, 24: 1, 27: 1, 28: 1, 30: 1, 31: 1}.get(k, 0)):
-                scores(*score_steps[done])
-                done = done + 1
+            for place, score_group, c in placed:
+                if place == k:
+                    scores(score_group, c)
+
         last = len(WIDTHS) - 1
         values = k_op[last][0]
-        k_op[last][1:] = [tile([P, HALVES * BLOCK], U32, "last_w"), tile([P, HALVES * BLOCK], U8, "last_s")]
+        k_op[last][1:] = [tile([P, HALVES * STEP], U32, "last_w"), tile([P, HALVES * STEP], U8, "last_s")]
         for h in range(HALVES):
-            cols = slice(h * BLOCK, (h + 1) * BLOCK)
+            cols = slice(h * STEP, (h + 1) * STEP)
             nc.vector.quantize_mx(
                 out=k_op[last][1][:, cols].bitcast(FP8X4), scales=k_op[last][2][:, cols],
                 in_=values[:, h * BANK : (h + 1) * BANK],
             )
-        for g, c in score_steps[done:-2]:
-            scores(g, c)
-        last_banks = [take_bank()[:, : GROUP // P * BLOCK] for c in range(M // GROUP)]
+        for c in range(M // GROUP):
+            scores(last - 1, c)
+        last_banks = [take_bank()[:, : GROUP // P * STEP] for c in range(M // GROUP)]
         for h in range(HALVES):
             for c in range(M // GROUP):
-                for slot in range(GROUP // P):
-                    score_pass(last_banks[c], last, c, slot, h, h == 0 and slot == 0, h == 1 and slot == 1)
+                for a in range(GROUP // P):
+                    score_pass(last_banks[c], last, c, a, h, (h, a) == (0, 0), (h, a) == (HALVES - 1, GROUP // P - 1))
         for c in range(M // GROUP):
             store(last_banks[c], last, c, c == 1)

@@ -42,7 +42,7 @@ STEPS_PER_GROUP = HALVES * GROUP // STEP
 WARM_UP_PASSES = 7
 QUERIES_AT = (13, 14)
 EARLY_GROUPS = 4
-SCORES_FROM = 16
+SCORES_FROM = 20
 SCORE_LAG = 4
 SHARE_FROM = 31
 SHARE_OF, SHARE = 5, (2, 4)
@@ -115,7 +115,8 @@ def tile_list_kvt_no_scale_kernel(
         def operand(width, name):
             return [tile([P, PACK * width], BF16, name + "_bf"), name]
 
-        x_op = operand(M, "x")
+        x_bf = []
+        x_op = [None, None, None]
         wq_op = [operand(PASS, "wq%d" % h) for h in range(HALVES)]
         q_op = [operand(HALVES * GROUP, "q%d" % c) for c in range(M // GROUP)]
         k_op = [operand(HALVES * width, "k%d" % g) for g, width in enumerate(WIDTHS)]
@@ -132,9 +133,21 @@ def tile_list_kvt_no_scale_kernel(
                 raw[:].rearrange("p (h c t e) -> p h t c e", h=HALVES, t=PACK, e=words_per_run),
             )
 
-        def round_x():
-            dst = x_op[0][:].rearrange("p (m code) -> p m code", code=PACK)
-            nc.gpsimd.tensor_scalar(dst, x_raw[:].rearrange("p code m -> p m code"), 1.0, 0.0, MULT, ADD)
+        def round_x(c, after=None):
+            x_bf.append(tile([P, PACK * GROUP], BF16, "x_bf%d" % c, after))
+            src = x_raw[:, :, c * GROUP : (c + 1) * GROUP]
+            if c == 0:
+                dst = x_bf[c][:].rearrange("p (m code) -> p m code", code=PACK)
+                nc.gpsimd.tensor_scalar(dst, src.rearrange("p code m -> p m code"), 1.0, 0.0, MULT, ADD)
+            else:
+                dst = x_bf[c][:].rearrange("p (n i code) -> p n code i", i=RUN, code=PACK)
+                nc.vector.tensor_copy(dst, src.rearrange("p code (n i) -> p n code i", i=RUN))
+
+        def quantise_x(after):
+            x_op[1:] = [tile([P, M], U32, "x_w", after), tile([P, M], U8, "x_s")]
+            for c in range(M // GROUP):
+                cols = slice(c * GROUP, (c + 1) * GROUP)
+                nc.vector.quantize_mx(out=x_op[1][:, cols].bitcast(FP8X4), scales=x_op[2][:, cols], in_=x_bf[c][:])
 
         def round_wq(h):
             dst = wq_op[h][0][:].rearrange("p (t c i code) -> p t c code i", t=PACK, i=RUN, code=PACK)
@@ -234,23 +247,24 @@ def tile_list_kvt_no_scale_kernel(
         move_scales(1)
         gather_words(0)
         gather_words(1)
-        round_x()
+        round_x(0)
 
         key_steps = [(g, step) for g, width in enumerate(WIDTHS) for step in range(HALVES * width // STEP)]
         last_key_step = len(key_steps) - 1
         early = [(g, c) for g in range(EARLY_GROUPS) for c in range(M // GROUP)]
         early[1:3] = [early[2], early[1]]
-        placed = [(SCORES_FROM + min(n, n // 2 + 1), g, c) for n, (g, c) in enumerate(early)]
+        placed = [(SCORES_FROM + n // 2, g, c) for n, (g, c) in enumerate(early)]
         for g in range(EARLY_GROUPS, WIDTHS.index(STEP)):
             for c in range(M // GROUP):
                 behind = (g + 1) * STEPS_PER_GROUP - 1 + SCORE_LAG + c
                 placed.append((min(behind, last_key_step), g, c))
 
         for k, (g, step) in enumerate(key_steps):
-            keys(g, step, k < BANKS and k % 2 == 1)
+            keys(g, step, k < BANKS - 1 and k % 2 == 1)
             if k == BANKS - 1:
+                round_x(1, "got_w0")
                 round_wq(0)
-                quantise(x_op, "wq_raw0")
+                quantise_x("wq_raw0")
                 quantise(wq_op[0])
                 round_wq(1)
                 quantise(k_op[0], "wq_raw1")
@@ -287,10 +301,22 @@ def tile_list_kvt_no_scale_kernel(
             )
         for c in range(M // GROUP):
             scores(last - 1, c)
-        last_banks = [take_bank()[:, : GROUP // P * STEP] for c in range(M // GROUP)]
+        last_banks = [take_bank()[:, :STEP] for a in range(M // P)]
         for h in range(HALVES):
-            for c in range(M // GROUP):
-                for a in range(GROUP // P):
-                    score_pass(last_banks[c], last, c, a, h, (h, a) == (0, 0), (h, a) == (HALVES - 1, GROUP // P - 1))
-        for c in range(M // GROUP):
-            store(last_banks[c], last, c, c == 1)
+            for a in range(M // P):
+                c, part = divmod(a, GROUP // P)
+                rows = slice(h * GROUP + part * P, h * GROUP + (part + 1) * P)
+                cols = slice(h * STEP, (h + 1) * STEP)
+                nc.tensor.matmul_mx(
+                    out=last_banks[a], lhsT=q_op[c][1][:, rows].bitcast(FP8X4), lhsT_scale=q_op[c][2][:, rows],
+                    rhs=k_op[last][1][:, cols].bitcast(FP8X4), rhs_scale=k_op[last][2][:, cols],
+                    start=h == 0, stop=h == HALVES - 1,
+                )
+        result = [tile([P, 2 * STEP], F32, "last%d" % n) for n in range(2)]
+        for a in range(M // P):
+            part = result[a % 2][:, a // 2 * STEP : (a // 2 + 1) * STEP]
+            if a % 2:
+                nc.vector.tensor_scalar(part, last_banks[a], SCORE_SCALE, None, MULT)
+            else:
+                nc.scalar.activation(part, last_banks[a], COPY, scale=SCORE_SCALE)
+            nc.sync.dma_start(out_tiles[:, a, FIRSTS[last] :], part)

@@ -39,8 +39,9 @@ WIDTHS = [GROUP] * 7 + [STEP] * 2
 FIRSTS = [sum(WIDTHS[:g]) for g in range(len(WIDTHS))]
 STEPS_PER_GROUP = HALVES * GROUP // STEP
 
-WARM_UP_PASSES = 7
-QUERIES_AT = (13, 14)
+WARM_UP_PASSES = 5
+KEEP_WARM_PASSES = 2
+QUERIES_AT = (13, 13, 13, 14, 15, 15, 15, 15)
 EARLY_GROUPS = 4
 SCORES_FROM = 20
 SCORE_LAG = 4
@@ -251,6 +252,7 @@ def tile_list_kvt_no_scale_kernel(
 
         key_steps = [(g, step) for g, width in enumerate(WIDTHS) for step in range(HALVES * width // STEP)]
         last_key_step = len(key_steps) - 1
+        query_steps = [(h, c, part) for h in range(HALVES) for c in range(M // GROUP) for part in range(GROUP // STEP)]
         early = [(g, c) for g in range(EARLY_GROUPS) for c in range(M // GROUP)]
         early[1:3] = [early[2], early[1]]
         placed = [(SCORES_FROM + n // 2, g, c) for n, (g, c) in enumerate(early)]
@@ -270,12 +272,17 @@ def tile_list_kvt_no_scale_kernel(
                 quantise(k_op[0], "wq_raw1")
                 quantise(wq_op[1])
                 gather_words(2, "wq1_bf")
-            if k in QUERIES_AT:
-                h = QUERIES_AT.index(k)
-                for c in range(M // GROUP):
-                    for part in range(GROUP // STEP):
-                        queries(c, h, part, (h, c, part) == (1, 1, 1))
-                    if (h, c) == (1, 0):
+            if k == QUERIES_AT[-1]:
+                for n in range(KEEP_WARM_PASSES):
+                    nc.tensor.matmul_mx(
+                        out=banks[len(taken) % BANKS][:],
+                        lhsT=k_op[0][1][:, :P].bitcast(FP8X4), lhsT_scale=k_op[0][2][:, :P],
+                        rhs=k_op[0][1][:].bitcast(FP8X4), rhs_scale=k_op[0][2][:], start=True, stop=True,
+                    )
+            for place, (h, c, part) in zip(QUERIES_AT, query_steps):
+                if place == k:
+                    queries(c, h, part, (h, c, part) == query_steps[-1])
+                    if (h, c, part) == (1, 0, 1):
                         quantise(q_op[0])
             if k == QUERIES_AT[-1]:
                 quantise(k_op[1], "q0_bf")
@@ -301,22 +308,10 @@ def tile_list_kvt_no_scale_kernel(
             )
         for c in range(M // GROUP):
             scores(last - 1, c)
-        last_banks = [take_bank()[:, :STEP] for a in range(M // P)]
+        last_banks = [take_bank()[:, : GROUP // P * STEP] for c in range(M // GROUP)]
         for h in range(HALVES):
-            for a in range(M // P):
-                c, part = divmod(a, GROUP // P)
-                rows = slice(h * GROUP + part * P, h * GROUP + (part + 1) * P)
-                cols = slice(h * STEP, (h + 1) * STEP)
-                nc.tensor.matmul_mx(
-                    out=last_banks[a], lhsT=q_op[c][1][:, rows].bitcast(FP8X4), lhsT_scale=q_op[c][2][:, rows],
-                    rhs=k_op[last][1][:, cols].bitcast(FP8X4), rhs_scale=k_op[last][2][:, cols],
-                    start=h == 0, stop=h == HALVES - 1,
-                )
-        result = [tile([P, 2 * STEP], F32, "last%d" % n) for n in range(2)]
-        for a in range(M // P):
-            part = result[a % 2][:, a // 2 * STEP : (a // 2 + 1) * STEP]
-            if a % 2:
-                nc.vector.tensor_scalar(part, last_banks[a], SCORE_SCALE, None, MULT)
-            else:
-                nc.scalar.activation(part, last_banks[a], COPY, scale=SCORE_SCALE)
-            nc.sync.dma_start(out_tiles[:, a, FIRSTS[last] :], part)
+            for c in range(M // GROUP):
+                for a in range(GROUP // P):
+                    score_pass(last_banks[c], last, c, a, h, (h, a) == (0, 0), (h, a) == (HALVES - 1, GROUP // P - 1))
+        for c in range(M // GROUP):
+            store(last_banks[c], last, c, c == 1)

@@ -41,12 +41,16 @@ STEPS_PER_GROUP = HALVES * GROUP // STEP
 
 WARM_UP_PASSES = 5
 KEEP_WARM_PASSES = 2
+EARLY_V = (2, 4, 6)
 QUERIES_AT = (13, 13, 13, 14, 15, 15, 15, 15)
 EARLY_GROUPS = 4
-SCORES_FROM = 20
-SCORE_LAG = 4
+SCORES_FROM = 17
+SCORE_LAG = 3
+RATE = (1, 1)
+LAG_C = 1
+LAST_AT = 31
 SHARE_FROM = 31
-SHARE_OF, SHARE = 5, (2, 4)
+SHARE_OF, SHARE = 7, (0, 2, 4)
 
 
 def tile_list_kvt_no_scale_kernel(
@@ -253,16 +257,15 @@ def tile_list_kvt_no_scale_kernel(
         key_steps = [(g, step) for g, width in enumerate(WIDTHS) for step in range(HALVES * width // STEP)]
         last_key_step = len(key_steps) - 1
         query_steps = [(h, c, part) for h in range(HALVES) for c in range(M // GROUP) for part in range(GROUP // STEP)]
-        early = [(g, c) for g in range(EARLY_GROUPS) for c in range(M // GROUP)]
-        early[1:3] = [early[2], early[1]]
-        placed = [(SCORES_FROM + n // 2, g, c) for n, (g, c) in enumerate(early)]
-        for g in range(EARLY_GROUPS, WIDTHS.index(STEP)):
-            for c in range(M // GROUP):
-                behind = (g + 1) * STEPS_PER_GROUP - 1 + SCORE_LAG + c
-                placed.append((min(behind, last_key_step), g, c))
+        score_steps = [(g, c) for g in range(WIDTHS.index(STEP)) for c in range(M // GROUP)]
+        score_steps[1:3] = [score_steps[2], score_steps[1]]
+        placed = []
+        for n, (g, c) in enumerate(score_steps):
+            made = (g + 1) * STEPS_PER_GROUP - 1
+            placed.append((min(max(SCORES_FROM + n * RATE[0] // RATE[1], made + SCORE_LAG + LAG_C * c), LAST_AT), g, c))
 
         for k, (g, step) in enumerate(key_steps):
-            keys(g, step, k < BANKS - 1 and k % 2 == 1)
+            keys(g, step, k in EARLY_V)
             if k == BANKS - 1:
                 round_x(1, "got_w0")
                 round_wq(0)

@@ -40,15 +40,11 @@ FIRSTS = [sum(WIDTHS[:g]) for g in range(len(WIDTHS))]
 STEPS_PER_GROUP = HALVES * GROUP // STEP
 
 WARM_UP_PASSES = 5
-KEEP_WARM_PASSES = 2
-EARLY_V = (2, 4, 6)
-QUERIES_AT = (13, 13, 13, 14, 15, 15, 15, 15)
+EARLY_ON_VECTOR = (2, 4, 6)
+QUERIES_AT = (13, 13, 13, 13, 14, 14, 14, 14)
 EARLY_GROUPS = 4
 SCORES_FROM = 17
 SCORE_LAG = 3
-RATE = (1, 1)
-LAG_C = 1
-LAST_AT = 31
 SHARE_FROM = 31
 SHARE_OF, SHARE = 7, (0, 2, 4)
 
@@ -69,8 +65,7 @@ def tile_list_kvt_no_scale_kernel(
         tab_s = tile([P, T], U8, "tab_s")
         wk_raw_w = tile([P, R // 2], I32, "wk_raw_w")
         wk_raw_s = tile([P, R // 4], I32, "wk_raw_s")
-        wk_w = tile([P, 2 * R], U8, "wk_w")
-        wk_s = tile([P, R], U8, "wk_s")
+        wk_half = []
         x_raw = tile([P, PACK, M], F32, "x_raw")
         wq_raw = [tile([P, PACK, PASS], F32, "wq_raw%d" % h) for h in range(HALVES)]
         key_scales = [tile([P, J // 2], U8, "plane%d" % n) for n in range(2)]
@@ -132,11 +127,14 @@ def tile_list_kvt_no_scale_kernel(
             got_w.append(tile([P, SLICE], U32, "got_w%d" % n, after))
             nc.vector.tensor_copy(got_w[n][:], tab_w[:].indirect(offsets[:, n * columns : (n + 1) * columns]))
 
-        def order_columns(ordered, raw, words_per_run):
-            nc.vector.tensor_copy(
-                ordered[:].bitcast(I32).rearrange("p (h t c e) -> p h t c e", h=HALVES, t=PACK, e=words_per_run),
-                raw[:].rearrange("p (h c t e) -> p h t c e", h=HALVES, t=PACK, e=words_per_run),
-            )
+        def order_columns(h, after=None):
+            wk_half.append(tile([P, 3 * PASS], U8, "wk%d" % h, after))
+            for ordered, raw, words in ((wk_half[h][:, : 2 * PASS], wk_raw_w, 2), (wk_half[h][:, 2 * PASS :], wk_raw_s, 1)):
+                width = PASS // RUN * words
+                nc.vector.tensor_copy(
+                    ordered.bitcast(I32).rearrange("p (t c e) -> p t c e", t=PACK, e=words),
+                    raw[:, h * width : (h + 1) * width].rearrange("p (c t e) -> p t c e", t=PACK, e=words),
+                )
 
         def round_x(c, after=None):
             x_bf.append(tile([P, PACK * GROUP], BF16, "x_bf%d" % c, after))
@@ -200,8 +198,8 @@ def tile_list_kvt_no_scale_kernel(
 
         def keys(g, step, on_vector):
             h, part = divmod(step, WIDTHS[g] // STEP)
-            starts = [h * PASS + t * P for t in range(PACK)]
-            weights = [(wk_w[:, 2 * r0 : 2 * (r0 + P)].bitcast(FP4X4), wk_s[:, r0 : r0 + P]) for r0 in starts]
+            words, scales = wk_half[h][:, : 2 * PASS], wk_half[h][:, 2 * PASS :]
+            weights = [(words[:, 2 * t * P : 2 * (t + 1) * P].bitcast(FP4X4), scales[:, t * P : (t + 1) * P]) for t in range(PACK)]
             n, at = divmod(FIRSTS[g] + part * STEP, SLICE)
             cols = slice(at, at + STEP)
             project(weights, got_w[n][:, cols], got_s[n][:, cols], k_op[g][0][:, step * BANK : (step + 1) * BANK], on_vector)
@@ -237,8 +235,7 @@ def tile_list_kvt_no_scale_kernel(
                     score_pass(bank, g, c, a, h, h == 0, h == HALVES - 1)
             store(bank, g, c, shared_out())
 
-        order_columns(wk_w, wk_raw_w, 2)
-        order_columns(wk_s, wk_raw_s, 1)
+        order_columns(0)
         gather_scales(1, 2)
 
         warm = operand(P, "warm")
@@ -252,20 +249,21 @@ def tile_list_kvt_no_scale_kernel(
         move_scales(1)
         gather_words(0)
         gather_words(1)
-        round_x(0)
+        order_columns(1, "parked0")
+        round_x(0, "wk_raw_s")
 
         key_steps = [(g, step) for g, width in enumerate(WIDTHS) for step in range(HALVES * width // STEP)]
-        last_key_step = len(key_steps) - 1
+        key_steps[2:6] = key_steps[4:6] + key_steps[2:4]
         query_steps = [(h, c, part) for h in range(HALVES) for c in range(M // GROUP) for part in range(GROUP // STEP)]
         score_steps = [(g, c) for g in range(WIDTHS.index(STEP)) for c in range(M // GROUP)]
         score_steps[1:3] = [score_steps[2], score_steps[1]]
         placed = []
         for n, (g, c) in enumerate(score_steps):
             made = (g + 1) * STEPS_PER_GROUP - 1
-            placed.append((min(max(SCORES_FROM + n * RATE[0] // RATE[1], made + SCORE_LAG + LAG_C * c), LAST_AT), g, c))
+            placed.append((max(SCORES_FROM + n, made + SCORE_LAG + c), g, c))
 
         for k, (g, step) in enumerate(key_steps):
-            keys(g, step, k in EARLY_V)
+            keys(g, step, k in EARLY_ON_VECTOR)
             if k == BANKS - 1:
                 round_x(1, "got_w0")
                 round_wq(0)
@@ -275,13 +273,6 @@ def tile_list_kvt_no_scale_kernel(
                 quantise(k_op[0], "wq_raw1")
                 quantise(wq_op[1])
                 gather_words(2, "wq1_bf")
-            if k == QUERIES_AT[-1]:
-                for n in range(KEEP_WARM_PASSES):
-                    nc.tensor.matmul_mx(
-                        out=banks[len(taken) % BANKS][:],
-                        lhsT=k_op[0][1][:, :P].bitcast(FP8X4), lhsT_scale=k_op[0][2][:, :P],
-                        rhs=k_op[0][1][:].bitcast(FP8X4), rhs_scale=k_op[0][2][:], start=True, stop=True,
-                    )
             for place, (h, c, part) in zip(QUERIES_AT, query_steps):
                 if place == k:
                     queries(c, h, part, (h, c, part) == query_steps[-1])

from contextlib import ExitStack

import concourse.mybir as mybir

K, R, M, T, J = 512, 1024, 512, 4096, 2048
FLOPS = 2 * K * R * M + 2 * K * R * J + 2 * R * M * J

F32 = mybir.dt.float32
BF16 = mybir.dt.bfloat16
I32 = mybir.dt.int32
U32 = mybir.dt.uint32
U16 = mybir.dt.uint16
U8 = mybir.dt.uint8
FP8X4 = mybir.dt.float8_e4m3fn_x4
FP4X4 = mybir.dt.float4_e2m1fn_x4
COPY = mybir.ActivationFunctionType.Copy
MULT = mybir.AluOpType.mult
ADD = mybir.AluOpType.add

P = 128
PACK = 4
PASS = P * PACK
HALVES = R // PASS
RUN = 4
QUADRANT = 32
SCALE_ROWS = 4
BLOCKS = PASS // 32
PARKED = P - BLOCKS
BANK = 512
BANKS = 8
STEP = BANK // PACK
GROUP = 256
SLICE = 512
OFFSETS_PER_COLUMN = 16
SCORE_SCALE = 0.03125
ALIGN = 256

WIDTHS = [GROUP] * 7 + [STEP] * 2
FIRSTS = [sum(WIDTHS[:g]) for g in range(len(WIDTHS))]
STEPS_PER_GROUP = HALVES * GROUP // STEP

WARM_UP_PASSES = 5
EARLY_ON_VECTOR = (2, 4, 6)
QUERIES_AT = (13, 13, 13, 13, 14, 14, 14, 14)
EARLY_GROUPS = 4
SCORES_FROM = 17
SCORE_LAG = 3
SHARE_FROM = 31
SHARE_OF, SHARE = 7, (0, 2, 4)


def tile_list_kvt_no_scale_kernel(
    tc, tab_words, tab_scales, x, wq, wk_words, wk_scales, offs, out
):
    nc = tc.nc
    with ExitStack() as ctx:
        keep = ctx.enter_context(tc.tile_pool(name="keep", bufs=1))
        psum = ctx.enter_context(tc.psum_pool(name="psum", bufs=1))

        def tile(shape, dtype, name, after=None):
            return keep.tile(shape, dtype, name=name, tag=after or name, align_bytes=ALIGN)

        offsets = keep.tile([P, J // OFFSETS_PER_COLUMN], U16, name="offsets")
        tab_w = tile([P, T], U32, "tab_w")
        tab_s = tile([P, T], U8, "tab_s")
        wk_raw_w = tile([P, R // 2], I32, "wk_raw_w")
        wk_raw_s = tile([P, R // 4], I32, "wk_raw_s")
        wk_half = []
        x_raw = tile([P, PACK, M], F32, "x_raw")
        wq_raw = [tile([P, PACK, PASS], F32, "wq_raw%d" % h) for h in range(HALVES)]
        key_scales = [tile([P, J // 2], U8, "plane%d" % n) for n in range(2)]

        nc.vector.memset(tab_s[:PARKED, :].bitcast(I32), 0)
        nc.gpsimd.memset(wk_raw_s[:], 0)
        for n in range(2):
            nc.gpsimd.memset(key_scales[n][:].bitcast(I32), 0)

        parked = []

        def gather_scales(n, pieces):
            parked.append(tile([P, J // 2], U8, "parked%d" % n))
            width = J // 2 // pieces
            columns = width // OFFSETS_PER_COLUMN
            for i in range(pieces):
                first = (n * pieces + i) * columns
                nc.vector.tensor_copy(
                    parked[n][:, i * width : (i + 1) * width], tab_s[:].indirect(offsets[:, first : first + columns])
                )

        def move_scales(n):
            for q in range(P // QUADRANT):
                nc.sync.dma_start(
                    key_scales[n][q * QUADRANT : q * QUADRANT + SCALE_ROWS, :].bitcast(I32),
                    parked[n][PARKED + q * SCALE_ROWS : PARKED + (q + 1) * SCALE_ROWS, :].bitcast(I32),
                )

        nc.sync.dma_start(offsets[:], offs)
        nc.sync.dma_start(tab_s[PARKED:, :].bitcast(I32), tab_scales[0].bitcast(I32))
        nc.sync.dma_start(wk_raw_w[:], wk_words[0].bitcast(I32))
        for row in range(SCALE_ROWS):
            nc.sync.dma_start(wk_raw_s[row:P:QUADRANT, :], wk_scales[0, row:BLOCKS:SCALE_ROWS, :].bitcast(I32))
        nc.sync.dma_start(tab_w[:].bitcast(I32), tab_words[0].rearrange("p t i -> p (t i)").bitcast(I32))
        gather_scales(0, 1)
        move_scales(0)
        nc.sync.dma_start(x_raw[:], x.rearrange("(p code) m -> p code m", code=PACK))
        for h in range(HALVES):
            columns_of_half = wq[:, h * PASS : (h + 1) * PASS]
            nc.sync.dma_start(wq_raw[h][:], columns_of_half.rearrange("(p code) r -> p code r", code=PACK))

        got_w = []
        got_s = [key_scales[n // 2][:, n % 2 * SLICE : (n % 2 + 1) * SLICE] for n in range(J // SLICE)]
        banks = [psum.tile([P, BANK], F32, name="bank%d" % b) for b in range(BANKS)]
        taken = []

        def operand(width, name):
            return [tile([P, PACK * width], BF16, name + "_bf"), name]

        x_bf = []
        x_op = [None, None, None]
        wq_op = [operand(PASS, "wq%d" % h) for h in range(HALVES)]
        q_op = [operand(HALVES * GROUP, "q%d" % c) for c in range(M // GROUP)]
        k_op = [operand(HALVES * width, "k%d" % g) for g, width in enumerate(WIDTHS)]
        out_tiles = out.rearrange("(a p) j -> p a j", p=P)

        def gather_words(n, after=None):
            columns = SLICE // OFFSETS_PER_COLUMN
            got_w.append(tile([P, SLICE], U32, "got_w%d" % n, after))
            nc.vector.tensor_copy(got_w[n][:], tab_w[:].indirect(offsets[:, n * columns : (n + 1) * columns]))

        def order_columns(h, after=None):
            wk_half.append(tile([P, 3 * PASS], U8, "wk%d" % h, after))
            for ordered, raw, words in ((wk_half[h][:, : 2 * PASS], wk_raw_w, 2), (wk_half[h][:, 2 * PASS :], wk_raw_s, 1)):
                width = PASS // RUN * words
                nc.vector.tensor_copy(
                    ordered.bitcast(I32).rearrange("p (t c e) -> p t c e", t=PACK, e=words),
                    raw[:, h * width : (h + 1) * width].rearrange("p (c t e) -> p t c e", t=PACK, e=words),
                )

        def round_x(c, after=None):
            x_bf.append(tile([P, PACK * GROUP], BF16, "x_bf%d" % c, after))
            src = x_raw[:, :, c * GROUP : (c + 1) * GROUP]
            if c == 0:
                dst = x_bf[c][:].rearrange("p (m code) -> p m code", code=PACK)
                nc.gpsimd.tensor_scalar(dst, src.rearrange("p code m -> p m code"), 1.0, 0.0, MULT, ADD)
            else:
                dst = x_bf[c][:].rearrange("p (n i code) -> p n code i", i=RUN, code=PACK)
                nc.vector.tensor_copy(dst, src.rearrange("p code (n i) -> p n code i", i=RUN))

        def quantise_x(after):
            x_op[1:] = [tile([P, M], U32, "x_w", after), tile([P, M], U8, "x_s")]
            for c in range(M // GROUP):
                cols = slice(c * GROUP, (c + 1) * GROUP)
                nc.vector.quantize_mx(out=x_op[1][:, cols].bitcast(FP8X4), scales=x_op[2][:, cols], in_=x_bf[c][:])

        def round_wq(h):
            dst = wq_op[h][0][:].rearrange("p (t c i code) -> p t c code i", t=PACK, i=RUN, code=PACK)
            src = wq_raw[h][:].rearrange("p code (c t i) -> p t c code i", t=PACK, i=RUN)
            nc.vector.tensor_copy(dst, src)

        def quantise(op, after=None):
            values, name = op
            words = tile([P, values.shape[1] // PACK], U32, name + "_w", after)
            scales = tile([P, values.shape[1] // PACK], U8, name + "_s")
            op[1:] = [words, scales]
            nc.vector.quantize_mx(out=words[:].bitcast(FP8X4), scales=scales[:], in_=values[:])

        def take_bank():
            taken.append(banks[len(taken) % BANKS])
            return taken[-1]

        def shared_out():
            return len(taken) > SHARE_FROM and len(taken) % SHARE_OF in SHARE

        def project(weights, moving_w, moving_s, values, on_vector):
            bank = take_bank()
            for t in range(PACK):
                nc.tensor.matmul_mx(
                    out=bank[:, t * STEP : (t + 1) * STEP], lhsT=weights[t][0], lhsT_scale=weights[t][1],
                    rhs=moving_w.bitcast(FP8X4), rhs_scale=moving_s, start=True, stop=True,
                )
            dst = values.rearrange("p (n t) -> p n t", t=PACK)
            src = bank[:].rearrange("p (t n) -> p n t", t=PACK)
            if on_vector or shared_out():
                nc.vector.tensor_copy(dst, src)
            elif len(taken) == 1:
                nc.scalar.activation(dst, src, COPY)
            else:
                nc.scalar.copy(dst, src)

        def queries(c, h, part, on_vector):
            weights = [
                (wq_op[h][1][:, t * P : (t + 1) * P].bitcast(FP8X4), wq_op[h][2][:, t * P : (t + 1) * P])
                for t in range(PACK)
            ]
            cols = slice(c * GROUP + part * STEP, c * GROUP + (part + 1) * STEP)
            step = h * (GROUP // STEP) + part
            project(weights, x_op[1][:, cols], x_op[2][:, cols], q_op[c][0][:, step * BANK : (step + 1) * BANK], on_vector)

        def keys(g, step, on_vector):
            h, part = divmod(step, WIDTHS[g] // STEP)
            words, scales = wk_half[h][:, : 2 * PASS], wk_half[h][:, 2 * PASS :]
            weights = [(words[:, 2 * t * P : 2 * (t + 1) * P].bitcast(FP4X4), scales[:, t * P : (t + 1) * P]) for t in range(PACK)]
            n, at = divmod(FIRSTS[g] + part * STEP, SLICE)
            cols = slice(at, at + STEP)
            project(weights, got_w[n][:, cols], got_s[n][:, cols], k_op[g][0][:, step * BANK : (step + 1) * BANK], on_vector)

        def score_pass(bank, g, c, a, h, start, stop):
            width = WIDTHS[g]
            rows = slice(h * GROUP + a * P, h * GROUP + (a + 1) * P)
            cols = slice(h * width, (h + 1) * width)
            nc.tensor.matmul_mx(
                out=bank[:, a * width : (a + 1) * width],
                lhsT=q_op[c][1][:, rows].bitcast(FP8X4), lhsT_scale=q_op[c][2][:, rows],
                rhs=k_op[g][1][:, cols].bitcast(FP8X4), rhs_scale=k_op[g][2][:, cols],
                start=start, stop=stop,
            )

        def store(bank, g, c, on_vector):
            width = WIDTHS[g]
            row_tiles = GROUP // P
            result = tile([P, row_tiles * width], F32, "res%d_%d" % (g, c))
            if on_vector:
                nc.vector.tensor_scalar(result[:], bank, SCORE_SCALE, None, MULT)
            else:
                nc.scalar.activation(result[:], bank, COPY, scale=SCORE_SCALE)
            nc.sync.dma_start(
                out_tiles[:, c * row_tiles : (c + 1) * row_tiles, FIRSTS[g] : FIRSTS[g] + width],
                result[:].rearrange("p (a j) -> p a j", a=row_tiles),
            )

        def scores(g, c):
            bank = take_bank()[:, : GROUP // P * WIDTHS[g]]
            for a in range(GROUP // P):
                for h in range(HALVES):
                    score_pass(bank, g, c, a, h, h == 0, h == HALVES - 1)
            store(bank, g, c, shared_out())

        order_columns(0)
        gather_scales(1, 2)

        warm = operand(P, "warm")
        nc.vector.memset(warm[0][:].bitcast(I32), 0)
        quantise(warm)
        for n in range(WARM_UP_PASSES):
            nc.tensor.matmul_mx(
                out=banks[-1][:], lhsT=warm[1][:].bitcast(FP8X4), lhsT_scale=warm[2][:],
                rhs=wk_raw_w[:, : BANK // 2].bitcast(FP4X4), rhs_scale=parked[1][:, :BANK], start=True, stop=True,
            )
        move_scales(1)
        gather_words(0)
        gather_words(1)
        order_columns(1, "parked0")
        round_x(0, "wk_raw_s")

        key_steps = [(g, step) for g, width in enumerate(WIDTHS) for step in range(HALVES * width // STEP)]
        key_steps[2:6] = key_steps[4:6] + key_steps[2:4]
        query_steps = [(h, c, part) for h in range(HALVES) for c in range(M // GROUP) for part in range(GROUP // STEP)]
        score_steps = [(g, c) for g in range(WIDTHS.index(STEP)) for c in range(M // GROUP)]
        score_steps[1:3] = [score_steps[2], score_steps[1]]
        placed = []
        for n, (g, c) in enumerate(score_steps):
            made = (g + 1) * STEPS_PER_GROUP - 1
            placed.append((max(SCORES_FROM + n, made + SCORE_LAG + c), g, c))

        for k, (g, step) in enumerate(key_steps):
            keys(g, step, k in EARLY_ON_VECTOR)
            if k == BANKS - 1:
                round_x(1, "got_w0")
                round_wq(0)
                quantise_x("wq_raw0")
                quantise(wq_op[0])
                round_wq(1)
                quantise(k_op[0], "wq_raw1")
                quantise(wq_op[1])
                gather_words(2, "wq1_bf")
            for place, (h, c, part) in zip(QUERIES_AT, query_steps):
                if place == k:
                    queries(c, h, part, (h, c, part) == query_steps[-1])
                    if (h, c, part) == (1, 0, 1):
                        quantise(q_op[0])
            if k == QUERIES_AT[-1]:
                quantise(k_op[1], "q0_bf")
                quantise(q_op[1])
                quantise(k_op[2], "q1_bf")
            if k == EARLY_GROUPS * STEPS_PER_GROUP:
                quantise(k_op[EARLY_GROUPS - 1], "k2_bf")
                gather_words(3, "k3_bf")
            if step == 0 and g > EARLY_GROUPS:
                quantise(k_op[g - 1])
            for place, score_group, c in placed:
                if place == k:
                    scores(score_group, c)

        last = len(WIDTHS) - 1
        values = k_op[last][0]
        k_op[last][1:] = [tile([P, HALVES * STEP], U32, "last_w"), tile([P, HALVES * STEP], U8, "last_s")]
        for h in range(HALVES):
            cols = slice(h * STEP, (h + 1) * STEP)
            nc.vector.quantize_mx(
                out=k_op[last][1][:, cols].bitcast(FP8X4), scales=k_op[last][2][:, cols],
                in_=values[:, h * BANK : (h + 1) * BANK],
            )
        for c in range(M // GROUP):
            scores(last - 1, c)
        last_banks = [take_bank()[:, : GROUP // P * STEP] for c in range(M // GROUP)]
        for h in range(HALVES):
            for c in range(M // GROUP):
                for a in range(GROUP // P):
                    score_pass(last_banks[c], last, c, a, h, (h, a) == (0, 0), (h, a) == (HALVES - 1, GROUP // P - 1))
        for c in range(M // GROUP):
            store(last_banks[c], last, c, c == 1)
